import numpy as np
import ml_dtypes


def mxq(x, axis, fmt="e4m3"):
    dtype, down = {"e4m3": (ml_dtypes.float8_e4m3fn, 7), "e5m2": (ml_dtypes.float8_e5m2, 14)}[fmt]
    v = np.moveaxis(np.asarray(x, np.float32).astype(ml_dtypes.bfloat16).astype(np.float64), axis, -1)
    blocks = v.reshape(v.shape[:-1] + (-1, 32))
    amax = np.abs(blocks).max(-1, keepdims=True)
    byte = np.maximum(np.where(amax > 0, np.frexp(amax)[1] - 1 + 127, 0) - down, 1)
    scale = np.exp2(byte - 127.0)
    codes = (blocks / scale).astype(np.float32).astype(dtype).astype(np.float64)
    return np.moveaxis((codes * scale).reshape(v.shape), -1, axis)


WIDE = False


def mx_kscale(k):
    if not WIDE:
        return np.ones(k)
    levels = np.array([10, -10, 5, -5, 0])
    if k % 512:
        return np.exp2(np.random.permutation(np.resize(levels, k // 32))).repeat(32)
    a = np.empty((k // 512, 16))
    for p in range(k // 512):
        a[p, :8] = np.random.permutation(np.resize(levels, 8))
        for g in range(8):
            far = levels[np.abs(levels - a[p, g]) >= 10]
            a[p, g + 8] = far[np.random.randint(len(far))]
    return np.exp2(a.ravel()).repeat(32)


BF16 = ml_dtypes.bfloat16


def bf(x):
    return np.asarray(x, np.float32).astype(BF16)


def f64(x):
    return np.asarray(x).astype(np.float64)


E2M1 = np.array([0.0, 0.5, 1.0, 1.5, 2.0, 3.0, 4.0, 6.0, -0.0, -0.5, -1.0, -1.5, -2.0, -3.0, -4.0, -6.0])


def pack_weight(w, fmt):
    k, n = w.shape
    w = f64(bf(w)).reshape(k // 32, 32, n)
    amax = np.abs(w).max(1)
    if fmt == "e4m3":
        byte = np.frexp(amax)[1] - 1 + 127 - 7
    else:
        mant, ex = np.frexp(amax / 6.0)
        byte = np.where(mant > 0.5, ex, ex - 1) + 127
    byte = np.clip(np.where(amax > 0, byte, 1), 1, 254)
    scaled = (w * np.exp2(127.0 - byte)[:, None, :]).reshape(k, n).astype(np.float32)
    by_word = np.ascontiguousarray(scaled.reshape(k // 512, 128, 4, n).transpose(0, 1, 3, 2))
    if fmt == "e4m3":
        words = by_word.astype(ml_dtypes.float8_e4m3fn).view(np.uint8)
    else:
        c = by_word.astype(ml_dtypes.float4_e2m1fn).view(np.uint8) & 0xF
        words = c[..., 0::2] | (c[..., 1::2] << 4)
    return np.ascontiguousarray(words), np.ascontiguousarray(byte.astype(np.uint8).reshape(k // 512, 16, n))


def unpack_weight(words, scales, fmt):
    g, p, n, _ = words.shape
    if fmt == "e4m3":
        vals = np.ascontiguousarray(words).view(ml_dtypes.float8_e4m3fn).astype(np.float64)
    else:
        nib = np.empty((g, p, n, 4), np.uint8)
        nib[..., 0::2] = words & 0xF
        nib[..., 1::2] = words >> 4
        vals = E2M1[nib]
    vals = vals * np.repeat(np.exp2(scales.astype(np.float64) - 127.0), 8, axis=1)[..., None]
    return vals.transpose(0, 1, 3, 2).reshape(g * 512, n)
def pack4(w):
    words, scales = pack_weight(w, "e2m1")
    return words.reshape(words.shape[0], 128, -1), scales


def unpack4(words, scales):
    return unpack_weight(words.reshape(words.shape[0], 128, -1, 2), scales, "e2m1")


M, N, K, S, H = 1024, 2048, 1024, 512, 512


def draw0():
    a = mx_kscale(K)
    b = mx_kscale(S)
    e = mx_kscale(M)
    u = np.random.standard_normal((M, K)) * a
    v = np.random.standard_normal((K, N)) / np.sqrt(2 * K) / a[:, None]
    c = np.random.standard_normal((M, S)) * b
    x = np.random.standard_normal((S, N)) / np.sqrt(2 * S) / b[:, None]
    d = (0.25 + np.abs(np.random.standard_normal(M))) * e
    w = np.random.standard_normal((M, H)) / np.sqrt(M) / e[:, None]
    x_words, x_scales = pack4(x)
    w_words, w_scales = pack4(w)
    return {"u": bf(u), "v": bf(v), "c": bf(c),
            "x_words": x_words, "x_scales": x_scales,
            "d": bf(d),
            "w_words": w_words, "w_scales": w_scales}


def core(u, v, c, x_words, x_scales, d, w_words, w_scales):
    x = unpack4(x_words, x_scales)
    w = unpack4(w_words, w_scales)
    full = mxq(f64(u), 1, "e4m3") @ mxq(f64(v), 0, "e4m3")
    skel = mxq(f64(c), 1, "e4m3") @ x
    r = full + skel
    err = r * r * f64(d)[:, None]
    return mxq(err, 0, "e4m3").T @ w


def e4m3fn_bytes(y):
    return np.clip(np.asarray(y, np.float64), -448.0, 448.0).astype(np.float32).astype(ml_dtypes.float8_e4m3fn).view(np.uint8)


def e4m3fn_values(b):
    return np.asarray(b, np.uint8).view(ml_dtypes.float8_e4m3fn).astype(np.float64)


def setup_inputs():
    d = draw0()
    x0 = np.asarray(d['v']).astype(np.float64)
    s = (np.max(np.abs(x0), axis=(1,), keepdims=True) / 448.0).astype(np.float32)
    out = {}
    for k, v in d.items():
        if k == 'v':
            out['v_bytes'] = e4m3fn_bytes(x0 / s.astype(np.float64))
            out['v_scale'] = s
        else:
            out[k] = v
    return out


def reference(u, v_bytes, v_scale, c, x_words, x_scales, d, w_words, w_scales):
    return core(u, e4m3fn_values(v_bytes) * v_scale.astype(np.float64), c, x_words, x_scales, d, w_words, w_scales)

@@ -1,0 +1,270 @@
+from contextlib import ExitStack
+
+import concourse.mybir as mybir
+from concourse.masks import make_identity
+
+M, N, K, S, H = 1024, 2048, 1024, 512, 512
+FLOPS = 2 * M * N * (K + S) + 2 * N * M * H
+
+F32 = mybir.dt.float32
+BF16 = mybir.dt.bfloat16
+I32 = mybir.dt.int32
+U32 = mybir.dt.uint32
+U8 = mybir.dt.uint8
+E4M3 = mybir.dt.float8_e4m3fn
+E4M3X4 = mybir.dt.float8_e4m3fn_x4
+E2M1X4 = mybir.dt.float4_e2m1fn_x4
+ACT = mybir.ActivationFunctionType
+ALU = mybir.AluOpType
+
+P = 128
+T4 = 4
+G = 2
+WIDTHS = (512, 512, 512, 256, 256)
+X_FIRST = 512
+
+
+def tile_skeleton_residual_contrasts_s3_kernel(tc, u, v_bytes, v_scale, c, x_words, x_scales, d, w_words, w_scales, out):
+    nc = tc.nc
+    starts = [sum(WIDTHS[:j]) for j in range(len(WIDTHS))]
+    nj = len(WIDTHS)
+
+    with ExitStack() as ctx:
+        keep = ctx.enter_context(tc.tile_pool(name="keep", bufs=1))
+        work = ctx.enter_context(tc.tile_pool(name="work", bufs=3))
+        psum = ctx.enter_context(tc.psum_pool(name="psum", bufs=1))
+        ctx.enter_context(tc.manual_schedule())
+
+        vs_sb = keep.tile([P, G, T4], F32, name="vs_sb")
+        nc.scalar.dma_start(out=vs_sb[:], in_=v_scale.rearrange("(g p t) o -> p g (t o)", p=P, t=T4))
+        d_sb = keep.tile([P, G, T4], BF16, name="d_sb")
+        nc.scalar.dma_start(out=d_sb[:], in_=d.rearrange("(g p t) -> p g t", p=P, t=T4))
+
+        xs_sb = keep.tile([P, N], U8, name="xs_sb", align_bytes=64)
+        ws_sb = keep.tile([P, G, H], U8, name="ws_sb", align_bytes=64)
+        nc.vector.memset(xs_sb[:].bitcast(I32), 0)
+        nc.vector.memset(ws_sb[:].rearrange("p g h -> p (g h)").bitcast(I32), 0)
+
+        v_rows = v_bytes.rearrange("(g p t) n -> g p t n", p=P, t=T4)
+        u_rows = u.rearrange("(g p t) k -> g p t k", p=P, t=T4)
+        c_rows = c.rearrange("(g p t) k -> g p t k", p=P, t=T4)
+        v_raw, u_raw, c_raw = {}, {}, {}
+
+        def load_v(j, g):
+            v_raw[j, g] = keep.tile([P, T4, WIDTHS[j]], U8, name="v_raw_%d_%d" % (j, g), align_bytes=64)
+            nc.sync.dma_start(out=v_raw[j, g][:], in_=v_rows[g][:, :, starts[j] : starts[j] + WIDTHS[j]])
+
+        def load_uc(a):
+            g, t0 = a // 2, 2 * (a % 2)
+            u_raw[a] = keep.tile([P, 2, K], BF16, name="u_raw_%d" % a, align_bytes=64)
+            nc.sync.dma_start(out=u_raw[a][:], in_=u_rows[g][:, t0 : t0 + 2, :])
+            c_raw[a] = keep.tile([P, 2, S], BF16, name="c_raw_%d" % a, align_bytes=64)
+            nc.sync.dma_start(out=c_raw[a][:], in_=c_rows[g][:, t0 : t0 + 2, :])
+
+        x_sb = keep.tile([P, 2 * N], U8, name="x_sb", align_bytes=64)
+
+        def load_x(lo, hi):
+            nc.sync.dma_start(out=x_sb[:, lo:hi].bitcast(I32), in_=x_words[0][:, lo:hi].bitcast(I32))
+
+        load_v(0, 0)
+        load_v(0, 1)
+        load_uc(0)
+        for q in range(4):
+            nc.sync.dma_start(out=xs_sb[32 * q : 32 * q + 4, :].bitcast(I32), in_=x_scales[0][4 * q : 4 * q + 4, :].bitcast(I32))
+        load_x(0, 2 * X_FIRST)
+        load_uc(1)
+        load_uc(2)
+        load_v(1, 0)
+        load_v(1, 1)
+        load_uc(3)
+        load_x(2 * X_FIRST, 2 * N)
+        for q in range(4):
+            nc.sync.dma_start(
+                out=ws_sb[32 * q : 32 * q + 4, :, :].rearrange("q g h -> q (g h)").bitcast(I32).rearrange("q (g h) -> q g h", g=G),
+                in_=w_scales.bitcast(I32).rearrange("g q h -> q g h")[4 * q : 4 * q + 4, :, :],
+            )
+        w_sb = keep.tile([P, G, 2 * H], U8, name="w_sb", align_bytes=64)
+        nc.sync.dma_start(out=w_sb[:], in_=w_words.rearrange("g p n -> p g n"))
+        for j in range(2, nj):
+            load_v(j, 0)
+            load_v(j, 1)
+
+        warm = keep.tile([P, 1], F32, name="warm")
+        nc.gpsimd.memset(warm[:], 0.0)
+        nc.scalar.activation(out=warm[:], in_=warm[:], func=ACT.Square)
+        ident = keep.tile([P, P], F32, name="ident")
+        make_identity(nc, ident[:])
+        half = keep.tile([P, G, T4], F32, name="half")
+        nc.gpsimd.memset(half[:], 0.5)
+        root = keep.tile([P, G, T4], F32, name="root")
+        nc.gpsimd.tensor_tensor(out=root[:], in0=d_sb[:], in1=half[:], op=ALU.pow)
+
+        u_codes, u_scl, c_codes, c_scl = {}, {}, {}, {}
+        banks = {}
+
+        def transposes_u(a, i):
+            words = u_raw[a][:, i, :].bitcast(F32)
+            bank = psum.tile([P, 4, P], F32, tag="r", bufs=5, name="ub")
+            for g in range(2):
+                for h in range(2):
+                    nc.tensor.transpose(bank[:, 2 * g + h, :], words[:, 256 * g + h : 256 * (g + 1) : 2], ident[:])
+            banks[a, i] = bank
+
+        def transposes_c(a):
+            bank = psum.tile([P, 4, P], F32, tag="r", bufs=5, name="cb")
+            for i in range(2):
+                words = c_raw[a][:, i, :].bitcast(F32)
+                for h in range(2):
+                    nc.tensor.transpose(bank[:, 2 * i + h, :], words[:, h:256:2], ident[:])
+            banks[a, 2] = bank
+
+        groups = {}
+
+        def copy_out(a, i, engine):
+            if i < 2:
+                if ("u", a) not in groups:
+                    groups["u", a] = work.tile([P, 2, 1024], BF16, tag="gu", bufs=3, name="gu", align_bytes=64)
+                dst = groups["u", a][:, i, :]
+            else:
+                groups["c", a] = work.tile([P, 1024], BF16, tag="gc", bufs=3, name="gc", align_bytes=64)
+                dst = groups["c", a][:]
+            dst = dst.bitcast(F32).rearrange("p (g r h) -> p g r h", g=2, h=2)
+            src = banks[a, i][:].rearrange("p (g h) r -> p g r h", g=2)
+            if engine == "S":
+                nc.scalar.copy(out=dst, in_=src)
+            else:
+                nc.vector.tensor_copy(out=dst, in_=src)
+
+        def quantize_u(a):
+            gu = groups["u", a]
+            u_codes[a] = keep.tile([P, 512], U32, name="u_codes_%d" % a, align_bytes=64)
+            u_scl[a] = keep.tile([P, 512], U8, name="u_scl_%d" % a, align_bytes=64)
+            nc.vector.quantize_mx(out=u_codes[a][:].bitcast(E4M3X4), scales=u_scl[a][:], in_=gu[:].rearrange("p i k -> p (i k)"))
+
+        def quantize_c(a):
+            gc = groups["c", a]
+            c_codes[a] = keep.tile([P, 256], U32, name="c_codes_%d" % a, align_bytes=64)
+            c_scl[a] = keep.tile([P, 256], U8, name="c_scl_%d" % a, align_bytes=64)
+            nc.vector.quantize_mx(out=c_codes[a][:].bitcast(E4M3X4), scales=c_scl[a][:], in_=gc[:])
+
+        v_wide, v_grp, v_codes, v_scl = {}, {}, {}, {}
+
+        def widen(j, g, t, engine):
+            if (j, g) not in v_wide:
+                v_wide[j, g] = work.tile([P, T4, WIDTHS[j]], BF16, tag="v_wide", bufs=5, name="v_wide", align_bytes=64)
+            src = v_raw[j, g][:, t, :].bitcast(E4M3)
+            dst = v_wide[j, g][:, t, :]
+            if engine == "S":
+                nc.scalar.activation(out=dst, in_=src, func=ACT.Copy, scale=vs_sb[:, g, t : t + 1])
+            else:
+                nc.vector.tensor_scalar(out=dst, in0=src, scalar1=vs_sb[:, g, t : t + 1], scalar2=None, op0=ALU.mult)
+
+        def interleave_v(j, g):
+            v_grp[j, g] = work.tile([P, WIDTHS[j], T4], BF16, tag="v_grp", bufs=3, name="v_grp", align_bytes=64)
+            nc.vector.tensor_copy(out=v_grp[j, g][:], in_=v_wide[j, g][:].rearrange("p t n -> p n t"))
+
+        def quantize_v(j, g):
+            v_codes[j, g] = keep.tile([P, WIDTHS[j]], U32, name="v_codes_%d_%d" % (j, g), align_bytes=64)
+            v_scl[j, g] = keep.tile([P, WIDTHS[j]], U8, name="v_scl_%d_%d" % (j, g), align_bytes=64)
+            nc.vector.quantize_mx(out=v_codes[j, g][:].bitcast(E4M3X4), scales=v_scl[j, g][:], in_=v_grp[j, g][:].rearrange("p n t -> p (n t)"))
+
+        r_banks, e_wide, e_grp, e_codes, e_scl = {}, {}, {}, {}, {}
+
+        def residual(j, g, t):
+            a, i = 2 * g + t // 2, t % 2
+            w = WIDTHS[j]
+            bank = psum.tile([P, w], F32, tag="r", bufs=5, name="rb")
+            r_banks[j, g, t] = bank
+            cc = slice(P * i, P * i + P)
+            step = w if w == 512 else P
+            for n in range(0, w, step):
+                nn = slice(n, n + step)
+                n0 = starts[j] + n
+                nc.tensor.matmul_mx(
+                    out=bank[:, nn], lhsT=c_codes[a][:, cc].bitcast(E4M3X4), lhsT_scale=c_scl[a][:, cc],
+                    rhs=x_sb[:, 2 * n0 : 2 * (n0 + step)].bitcast(E2M1X4), rhs_scale=xs_sb[:, n0 : n0 + step], start=True, stop=False)
+                for k in range(2):
+                    cu = slice(256 * i + P * k, 256 * i + P * k + P)
+                    nc.tensor.matmul_mx(
+                        out=bank[:, nn], lhsT=u_codes[a][:, cu].bitcast(E4M3X4), lhsT_scale=u_scl[a][:, cu],
+                        rhs=v_codes[j, k][:, nn].bitcast(E4M3X4), rhs_scale=v_scl[j, k][:, nn], start=False, stop=(k == 1))
+
+        def square(j, g, t):
+            if (j, g) not in e_wide:
+                e_wide[j, g] = work.tile([P, T4, WIDTHS[j]], BF16, tag="e_wide", bufs=4, name="e_wide", align_bytes=64)
+            nc.scalar.activation(out=e_wide[j, g][:, t, :], in_=r_banks[j, g, t][:], func=ACT.Square, scale=root[:, g, t : t + 1])
+
+        def interleave_e(j, g):
+            e_grp[j, g] = work.tile([P, WIDTHS[j], T4], BF16, tag="e_grp", bufs=3, name="e_grp", align_bytes=64)
+            nc.vector.tensor_copy(out=e_grp[j, g][:], in_=e_wide[j, g][:].rearrange("p t n -> p n t"))
+
+        def quantize_e(j, g):
+            e_codes[j, g] = work.tile([P, WIDTHS[j]], U32, tag="e_codes", bufs=8, name="e_codes", align_bytes=64)
+            e_scl[j, g] = work.tile([P, WIDTHS[j]], U8, tag="e_scl", bufs=8, name="e_scl", align_bytes=64)
+            nc.vector.quantize_mx(out=e_codes[j, g][:].bitcast(E4M3X4), scales=e_scl[j, g][:], in_=e_grp[j, g][:].rearrange("p n t -> p (n t)"))
+
+        o_banks = {}
+
+        def contrast(j, q):
+            bank = psum.tile([P, H], F32, tag="o", bufs=3, name="ob")
+            o_banks[j, q] = bank
+            cq = slice(P * q, P * q + P)
+            for g in range(G):
+                nc.tensor.matmul_mx(
+                    out=bank[:], lhsT=e_codes[j, g][:, cq].bitcast(E4M3X4), lhsT_scale=e_scl[j, g][:, cq],
+                    rhs=w_sb[:, g, :].bitcast(E2M1X4), rhs_scale=ws_sb[:, g, :], start=(g == 0), stop=(g == 1))
+
+        def store(j, q, engine):
+            o_sb = work.tile([P, H], F32, tag="o_sb", bufs=4, name="o_sb", align_bytes=64)
+            if engine == "S":
+                nc.scalar.copy(out=o_sb[:], in_=o_banks[j, q][:])
+            else:
+                nc.vector.tensor_copy(out=o_sb[:], in_=o_banks[j, q][:])
+            r0 = starts[j] + P * q
+            nc.sync.dma_start(out=out[r0 : r0 + P, :], in_=o_sb[:])
+
+        Q = {"headlen":1.77,"tr":1321.44,"cp":1197.25,"qu":733.44,"qc":882.26,"tr_a":203.98,"sq":81.28,"q0":1187.08,"q01":118.8,"wS":2178.96,"wgS":366.63,"wtS":-109.36,"wV":1620.55,"wgV":561.32,"wtV":-268.75,"iv":1157.9,"ivg":358.1,"qv":981.47,"qvg":511.74,"ie":672.62,"qe":795.11,"ct":1313.35,"ctq":165.99,"st":81.02,"wide":["SVSV","SSVV","SSVS","VSVV","VSSV","SSVV"],"copyeng":["SSS","SSS","SSV","VSV"]}
+        lengths = [w * (Q["headlen"] if j == 0 else 1.0) for j, w in enumerate(WIDTHS)]
+        at = [2 * sum(lengths[:j]) for j in range(nj + 1)]
+
+        def slot(j, g):
+            return at[j] + g * lengths[j]
+
+        steps = []
+
+        def add(key, fn, *args):
+            steps.append((key, len(steps), fn, args))
+
+        for a in range(4):
+            base = slot(0, a // 2) + (a % 2) * lengths[0] / 2
+            for i in range(3):
+                add(base - Q["tr"] - Q["tr_a"] * (3 - a) + i, transposes_u if i < 2 else transposes_c, *((a, i) if i < 2 else (a,)))
+                e = Q["copyeng"][a][i]
+                add(base - Q["cp"] - Q["tr_a"] * (3 - a) + i, copy_out, a, i, e)
+            add(base - Q["qu"] - Q["tr_a"] * (3 - a), quantize_u, a)
+            add(base - Q["qc"] - Q["tr_a"] * (3 - a), quantize_c, a)
+        for j in range(nj):
+            for g in range(G):
+                for t in range(T4):
+                    key = slot(j, g) + t * lengths[j] / 4
+                    add(key, residual, j, g, t)
+                    add(key + Q["sq"], square, j, g, t)
+                    e = Q["wide"][j][t]
+                    if j == 0:
+                        add(at[0] - 3000 + 1000 * g + t, widen, j, g, t, e)
+                    else:
+                        add(at[j] - Q["w" + e] + g * Q["wg" + e] + t * Q["wt" + e], widen, j, g, t, e)
+                if j == 0:
+                    add(at[0] - 2500 + 1000 * g, interleave_v, j, g)
+                    add(at[0] - Q["q0"] + Q["q01"] * g, quantize_v, j, g)
+                else:
+                    add(at[j] - Q["iv"] + g * Q["ivg"], interleave_v, j, g)
+                    add(at[j] - Q["qv"] + g * Q["qvg"], quantize_v, j, g)
+                add(slot(j, g + 1) + Q["ie"], interleave_e, j, g)
+                add(slot(j, g + 1) + Q["qe"], quantize_e, j, g)
+            for q in range(WIDTHS[j] // P):
+                key = at[j + 1] + Q["ct"] + q * Q["ctq"]
+                add(key, contrast, j, q)
+                add(key + Q["st"], store, j, q, "SV"[q % 2] if j == nj - 1 else "S")
+        for key, n, fn, args in sorted(steps, key=lambda s: (s[0], s[1])):
+            fn(*args)

@@ -20,8 +20,10 @@ ALU = mybir.AluOpType
 P = 128
 T4 = 4
 G = 2
-WIDTHS = (512, 512, 512, 256, 256)
+WIDTHS = (512, 512, 512, 512)
 X_FIRST = 512
+N_WARM = 7
+PARTS = (1, 1, 1, 2)
 
 
 def tile_skeleton_residual_contrasts_s3_kernel(tc, u, v_bytes, v_scale, c, x_words, x_scales, d, w_words, w_scales, out):
@@ -54,44 +56,59 @@ def tile_skeleton_residual_contrasts_s3_kernel(tc, u, v_bytes, v_scale, c, x_wor
             v_raw[j, g] = keep.tile([P, T4, WIDTHS[j]], U8, name="v_raw_%d_%d" % (j, g), align_bytes=64)
             nc.sync.dma_start(out=v_raw[j, g][:], in_=v_rows[g][:, :, starts[j] : starts[j] + WIDTHS[j]])
 
-        def load_uc(a):
+        def load_u(a, i):
+            g, t = a // 2, 2 * (a % 2) + i
+            u_raw[a, i] = keep.tile([P, K], BF16, name="u_raw_%d_%d" % (a, i), align_bytes=64)
+            nc.sync.dma_start(out=u_raw[a, i][:], in_=u_rows[g][:, t, :])
+
+        def load_c(a):
             g, t0 = a // 2, 2 * (a % 2)
-            u_raw[a] = keep.tile([P, 2, K], BF16, name="u_raw_%d" % a, align_bytes=64)
-            nc.sync.dma_start(out=u_raw[a][:], in_=u_rows[g][:, t0 : t0 + 2, :])
             c_raw[a] = keep.tile([P, 2, S], BF16, name="c_raw_%d" % a, align_bytes=64)
             nc.sync.dma_start(out=c_raw[a][:], in_=c_rows[g][:, t0 : t0 + 2, :])
 
         x_sb = keep.tile([P, 2 * N], U8, name="x_sb", align_bytes=64)
+        w_sb = keep.tile([P, G, 2 * H], U8, name="w_sb", align_bytes=64)
 
         def load_x(lo, hi):
             nc.sync.dma_start(out=x_sb[:, lo:hi].bitcast(I32), in_=x_words[0][:, lo:hi].bitcast(I32))
 
-        load_v(0, 0)
-        load_v(0, 1)
-        load_uc(0)
-        for q in range(4):
-            nc.sync.dma_start(out=xs_sb[32 * q : 32 * q + 4, :].bitcast(I32), in_=x_scales[0][4 * q : 4 * q + 4, :].bitcast(I32))
-        load_x(0, 2 * X_FIRST)
-        load_uc(1)
-        load_uc(2)
-        load_v(1, 0)
-        load_v(1, 1)
-        load_uc(3)
-        load_x(2 * X_FIRST, 2 * N)
-        for q in range(4):
-            nc.sync.dma_start(
-                out=ws_sb[32 * q : 32 * q + 4, :, :].rearrange("q g h -> q (g h)").bitcast(I32).rearrange("q (g h) -> q g h", g=G),
-                in_=w_scales.bitcast(I32).rearrange("g q h -> q g h")[4 * q : 4 * q + 4, :, :],
-            )
-        w_sb = keep.tile([P, G, 2 * H], U8, name="w_sb", align_bytes=64)
-        nc.sync.dma_start(out=w_sb[:], in_=w_words.rearrange("g p n -> p g n"))
-        for j in range(2, nj):
-            load_v(j, 0)
-            load_v(j, 1)
+        def load_xs():
+            for q in range(4):
+                nc.sync.dma_start(out=xs_sb[32 * q : 32 * q + 4, :].bitcast(I32), in_=x_scales[0][4 * q : 4 * q + 4, :].bitcast(I32))
+
+        def load_w():
+            for q in range(4):
+                nc.sync.dma_start(
+                    out=ws_sb[32 * q : 32 * q + 4, :, :].rearrange("q g h -> q (g h)").bitcast(I32).rearrange("q (g h) -> q g h", g=G),
+                    in_=w_scales.bitcast(I32).rearrange("g q h -> q g h")[4 * q : 4 * q + 4, :, :],
+                )
+            nc.sync.dma_start(out=w_sb[:], in_=w_words.rearrange("g p n -> p g n"))
+
+        Q = {"headlen":1.68,"tr":1206,"cp":975,"qu":408,"qc":537,"tr_a":174,"sq":130,"q0":1649,"q01":695,"wS":1810,"wgS":446,"wtS":102,"wV":1469,"wgV":371,"wtV":-79,"iv":1098,"ivg":308,"qv":1007,"qvg":515,"ie":555,"qe":791,"ct":1301,"ctq":140,"st":178,"wide":["SVVS","VSSV","SVVS","VSVS","VSSV","SSVV"],"vt":["VS","VS","SS","SS","VV","VV"],"last":["B2","B2","S","S"],"loads":["v00","u00","v01","u11","x0","u01","c0","u10","c1","u21","u20","xs","c2","v10","u30","u31","c3","v11","x1","v31","v21","w","v30","v20"],"copyeng":["SSS","SSS","SSS","VSS"]}
+        for name in Q["loads"]:
+            if name[0] == "v":
+                load_v(int(name[1]), int(name[2]))
+            elif name[0] == "u":
+                load_u(int(name[1]), int(name[2]))
+            elif name[0] == "c":
+                load_c(int(name[1]))
+            elif name == "xs":
+                load_xs()
+            elif name == "x0":
+                load_x(0, 2 * X_FIRST)
+            elif name == "x1":
+                load_x(2 * X_FIRST, 2 * N)
+            else:
+                load_w()
 
         warm = keep.tile([P, 1], F32, name="warm")
         nc.gpsimd.memset(warm[:], 0.0)
         nc.scalar.activation(out=warm[:], in_=warm[:], func=ACT.Square)
+        zero = keep.tile([P, 512], BF16, name="zero")
+        nc.vector.memset(zero[:], 0.0)
+        warm_bank = psum.tile([P, 512], F32, tag="o", bufs=3, name="warm_bank")
+        for x in range(N_WARM):
+            nc.tensor.matmul(warm_bank[:], lhsT=zero[:, :P], rhs=zero[:], start=True, stop=True)
         ident = keep.tile([P, P], F32, name="ident")
         make_identity(nc, ident[:])
         half = keep.tile([P, G, T4], F32, name="half")
@@ -103,7 +120,7 @@ def tile_skeleton_residual_contrasts_s3_kernel(tc, u, v_bytes, v_scale, c, x_wor
         banks = {}
 
         def transposes_u(a, i):
-            words = u_raw[a][:, i, :].bitcast(F32)
+            words = u_raw[a, i][:].bitcast(F32)
             bank = psum.tile([P, 4, P], F32, tag="r", bufs=5, name="ub")
             for g in range(2):
                 for h in range(2):
@@ -194,36 +211,48 @@ def tile_skeleton_residual_contrasts_s3_kernel(tc, u, v_bytes, v_scale, c, x_wor
                 e_wide[j, g] = work.tile([P, T4, WIDTHS[j]], BF16, tag="e_wide", bufs=4, name="e_wide", align_bytes=64)
             nc.scalar.activation(out=e_wide[j, g][:, t, :], in_=r_banks[j, g, t][:], func=ACT.Square, scale=root[:, g, t : t + 1])
 
-        def interleave_e(j, g):
-            e_grp[j, g] = work.tile([P, WIDTHS[j], T4], BF16, tag="e_grp", bufs=3, name="e_grp", align_bytes=64)
-            nc.vector.tensor_copy(out=e_grp[j, g][:], in_=e_wide[j, g][:].rearrange("p t n -> p n t"))
+        def interleave_e(j, g, h):
+            ew = WIDTHS[j] // PARTS[j]
+            e_grp[j, g, h] = work.tile([P, ew, T4], BF16, tag="e_grp", bufs=3, name="e_grp", align_bytes=64)
+            nc.vector.tensor_copy(out=e_grp[j, g, h][:], in_=e_wide[j, g][:, :, h * ew : (h + 1) * ew].rearrange("p t n -> p n t"))
 
-        def quantize_e(j, g):
-            e_codes[j, g] = work.tile([P, WIDTHS[j]], U32, tag="e_codes", bufs=8, name="e_codes", align_bytes=64)
-            e_scl[j, g] = work.tile([P, WIDTHS[j]], U8, tag="e_scl", bufs=8, name="e_scl", align_bytes=64)
-            nc.vector.quantize_mx(out=e_codes[j, g][:].bitcast(E4M3X4), scales=e_scl[j, g][:], in_=e_grp[j, g][:].rearrange("p n t -> p (n t)"))
+        def quantize_e(j, g, h):
+            ew = WIDTHS[j] // PARTS[j]
+            e_codes[j, g, h] = work.tile([P, ew], U32, tag="e_codes", bufs=8, name="e_codes", align_bytes=64)
+            e_scl[j, g, h] = work.tile([P, ew], U8, tag="e_scl", bufs=8, name="e_scl", align_bytes=64)
+            nc.vector.quantize_mx(out=e_codes[j, g, h][:].bitcast(E4M3X4), scales=e_scl[j, g, h][:], in_=e_grp[j, g, h][:].rearrange("p n t -> p (n t)"))
 
         o_banks = {}
 
         def contrast(j, q):
             bank = psum.tile([P, H], F32, tag="o", bufs=3, name="ob")
             o_banks[j, q] = bank
-            cq = slice(P * q, P * q + P)
+            h, q0 = divmod(q, WIDTHS[j] // PARTS[j] // P)
+            cq = slice(P * q0, P * q0 + P)
             for g in range(G):
                 nc.tensor.matmul_mx(
-                    out=bank[:], lhsT=e_codes[j, g][:, cq].bitcast(E4M3X4), lhsT_scale=e_scl[j, g][:, cq],
+                    out=bank[:], lhsT=e_codes[j, g, h][:, cq].bitcast(E4M3X4), lhsT_scale=e_scl[j, g, h][:, cq],
                     rhs=w_sb[:, g, :].bitcast(E2M1X4), rhs_scale=ws_sb[:, g, :], start=(g == 0), stop=(g == 1))
 
         def store(j, q, engine):
-            o_sb = work.tile([P, H], F32, tag="o_sb", bufs=4, name="o_sb", align_bytes=64)
-            if engine == "S":
-                nc.scalar.copy(out=o_sb[:], in_=o_banks[j, q][:])
-            else:
-                nc.vector.tensor_copy(out=o_sb[:], in_=o_banks[j, q][:])
             r0 = starts[j] + P * q
-            nc.sync.dma_start(out=out[r0 : r0 + P, :], in_=o_sb[:])
+            if len(engine) == 1:
+                o_sb = work.tile([P, H], F32, tag="o_sb", bufs=4, name="o_sb", align_bytes=64)
+                if engine == "S":
+                    nc.scalar.copy(out=o_sb[:], in_=o_banks[j, q][:])
+                else:
+                    nc.vector.tensor_copy(out=o_sb[:], in_=o_banks[j, q][:])
+                nc.sync.dma_start(out=out[r0 : r0 + P, :], in_=o_sb[:])
+            else:
+                for h in range(2):
+                    o_half = work.tile([P, H // 2], F32, tag="o_half", bufs=4, name="o_half", align_bytes=64)
+                    cols = slice(h * H // 2, (h + 1) * H // 2)
+                    if h == 0:
+                        nc.scalar.copy(out=o_half[:], in_=o_banks[j, q][:, cols])
+                    else:
+                        nc.vector.tensor_copy(out=o_half[:], in_=o_banks[j, q][:, cols])
+                    nc.sync.dma_start(out=out[r0 : r0 + P, cols], in_=o_half[:])
 
-        Q = {"headlen":1.77,"tr":1321.44,"cp":1197.25,"qu":733.44,"qc":882.26,"tr_a":203.98,"sq":81.28,"q0":1187.08,"q01":118.8,"wS":2178.96,"wgS":366.63,"wtS":-109.36,"wV":1620.55,"wgV":561.32,"wtV":-268.75,"iv":1157.9,"ivg":358.1,"qv":981.47,"qvg":511.74,"ie":672.62,"qe":795.11,"ct":1313.35,"ctq":165.99,"st":81.02,"wide":["SVSV","SSVV","SSVS","VSVV","VSSV","SSVV"],"copyeng":["SSS","SSS","SSV","VSV"]}
         lengths = [w * (Q["headlen"] if j == 0 else 1.0) for j, w in enumerate(WIDTHS)]
         at = [2 * sum(lengths[:j]) for j in range(nj + 1)]
 
@@ -260,11 +289,13 @@ def tile_skeleton_residual_contrasts_s3_kernel(tc, u, v_bytes, v_scale, c, x_wor
                 else:
                     add(at[j] - Q["iv"] + g * Q["ivg"], interleave_v, j, g)
                     add(at[j] - Q["qv"] + g * Q["qvg"], quantize_v, j, g)
-                add(slot(j, g + 1) + Q["ie"], interleave_e, j, g)
-                add(slot(j, g + 1) + Q["qe"], quantize_e, j, g)
+                for h in range(PARTS[j]):
+                    dh = h * lengths[j] / PARTS[j]
+                    add(slot(j, g + 1) + Q["ie"] + dh, interleave_e, j, g, h)
+                    add(slot(j, g + 1) + Q["qe"] + dh, quantize_e, j, g, h)
             for q in range(WIDTHS[j] // P):
                 key = at[j + 1] + Q["ct"] + q * Q["ctq"]
                 add(key, contrast, j, q)
-                add(key + Q["st"], store, j, q, "SV"[q % 2] if j == nj - 1 else "S")
+                add(key + Q["st"], store, j, q, "S" if j < nj - 1 else Q["last"][q])
         for key, n, fn, args in sorted(steps, key=lambda s: (s[0], s[1])):
             fn(*args)

@@ -22,7 +22,7 @@ T4 = 4
 G = 2
 WIDTHS = (512, 512, 512, 512)
 X_FIRST = 512
-N_WARM = 7
+N_WARM = 3
 PARTS = (1, 1, 1, 2)
 
 
@@ -84,7 +84,7 @@ def tile_skeleton_residual_contrasts_s3_kernel(tc, u, v_bytes, v_scale, c, x_wor
                 )
             nc.sync.dma_start(out=w_sb[:], in_=w_words.rearrange("g p n -> p g n"))
 
-        Q = {"headlen":1.68,"tr":1206,"cp":975,"qu":408,"qc":537,"tr_a":174,"sq":130,"q0":1649,"q01":695,"wS":1810,"wgS":446,"wtS":102,"wV":1469,"wgV":371,"wtV":-79,"iv":1098,"ivg":308,"qv":1007,"qvg":515,"ie":555,"qe":791,"ct":1301,"ctq":140,"st":178,"wide":["SVVS","VSSV","SVVS","VSVS","VSSV","SSVV"],"vt":["VS","VS","SS","SS","VV","VV"],"last":["B2","B2","S","S"],"loads":["v00","u00","v01","u11","x0","u01","c0","u10","c1","u21","u20","xs","c2","v10","u30","u31","c3","v11","x1","v31","v21","w","v30","v20"],"copyeng":["SSS","SSS","SSS","VSS"]}
+        Q = {"headlen":1.64,"tr":1169,"cp":847,"qu":335,"qc":363,"tr_a":101,"sq":121,"q0":1136,"q01":930,"wS":1773,"wgS":473,"wtS":125,"wV":1445,"wgV":325,"wtV":105,"iv":1065,"ivg":489,"qv":797,"qvg":335,"ie":607,"qe":810,"ct":1305,"ctq":125,"st":167,"wide":["SSSV","SSSS","VVVV","SSSS","VSSV","SSVV"],"vt":["VS","SV","SS","VS"],"last":["B2","B2","S","S"],"loads":["xs","v00","v01","u00","u01","c0","u10","u11","c1","u20","u21","c2","x0","v10","u30","u31","c3","v11","v21","v30","v20","v31","x1","w"],"sp":-1324,"speng":["VSS","SVV","SVS","SSS"],"copyeng":["SSV","SSS","SSS","VVS"]}
         for name in Q["loads"]:
             if name[0] == "v":
                 load_v(int(name[1]), int(name[2]))
@@ -168,22 +168,26 @@ def tile_skeleton_residual_contrasts_s3_kernel(tc, u, v_bytes, v_scale, c, x_wor
 
         def widen(j, g, t, engine):
             if (j, g) not in v_wide:
-                v_wide[j, g] = work.tile([P, T4, WIDTHS[j]], BF16, tag="v_wide", bufs=5, name="v_wide", align_bytes=64)
+                v_wide[j, g] = work.tile([P, T4 * WIDTHS[j]], BF16, tag="v_wide", bufs=5, name="v_wide", align_bytes=64)
             src = v_raw[j, g][:, t, :].bitcast(E4M3)
-            dst = v_wide[j, g][:, t, :]
             if engine == "S":
+                dst = v_wide[j, g][:].rearrange("p (t n) -> p t n", t=T4)[:, t, :]
                 nc.scalar.activation(out=dst, in_=src, func=ACT.Copy, scale=vs_sb[:, g, t : t + 1])
             else:
+                dst = v_wide[j, g][:].rearrange("p (r n e) -> p r n e", r=2, e=2)[:, t // 2, :, t % 2]
                 nc.vector.tensor_scalar(out=dst, in0=src, scalar1=vs_sb[:, g, t : t + 1], scalar2=None, op0=ALU.mult)
 
         def interleave_v(j, g):
-            v_grp[j, g] = work.tile([P, WIDTHS[j], T4], BF16, tag="v_grp", bufs=3, name="v_grp", align_bytes=64)
-            nc.vector.tensor_copy(out=v_grp[j, g][:], in_=v_wide[j, g][:].rearrange("p t n -> p n t"))
+            v_grp[j, g] = work.tile([P, T4 * WIDTHS[j]], BF16, tag="v_grp", bufs=3, name="v_grp", align_bytes=64)
+            if Q["vt"][j][g] == "S":
+                nc.vector.tensor_copy(out=v_grp[j, g][:].rearrange("p (n t) -> p n t", t=T4), in_=v_wide[j, g][:].rearrange("p (t n) -> p n t", t=T4))
+            else:
+                nc.vector.tensor_copy(out=v_grp[j, g][:].bitcast(F32).rearrange("p (n r) -> p n r", r=2), in_=v_wide[j, g][:].bitcast(F32).rearrange("p (r n) -> p n r", r=2))
 
         def quantize_v(j, g):
             v_codes[j, g] = keep.tile([P, WIDTHS[j]], U32, name="v_codes_%d_%d" % (j, g), align_bytes=64)
             v_scl[j, g] = keep.tile([P, WIDTHS[j]], U8, name="v_scl_%d_%d" % (j, g), align_bytes=64)
-            nc.vector.quantize_mx(out=v_codes[j, g][:].bitcast(E4M3X4), scales=v_scl[j, g][:], in_=v_grp[j, g][:].rearrange("p n t -> p (n t)"))
+            nc.vector.quantize_mx(out=v_codes[j, g][:].bitcast(E4M3X4), scales=v_scl[j, g][:], in_=v_grp[j, g][:])
 
         r_banks, e_wide, e_grp, e_codes, e_scl = {}, {}, {}, {}, {}
 
@@ -278,7 +282,7 @@ def tile_skeleton_residual_contrasts_s3_kernel(tc, u, v_bytes, v_scale, c, x_wor
                     key = slot(j, g) + t * lengths[j] / 4
                     add(key, residual, j, g, t)
                     add(key + Q["sq"], square, j, g, t)
-                    e = Q["wide"][j][t]
+                    e = Q["vt"][j][g]
                     if j == 0:
                         add(at[0] - 3000 + 1000 * g + t, widen, j, g, t, e)
                     else:

@@ -42,8 +42,10 @@ def tile_skeleton_residual_contrasts_s3_kernel(tc, u, v_bytes, v_scale, c, x_wor
         d_sb = keep.tile([P, G, T4], BF16, name="d_sb")
         nc.scalar.dma_start(out=d_sb[:], in_=d.rearrange("(g p t) -> p g t", p=P, t=T4))
 
-        xs_sb = keep.tile([P, N], U8, name="xs_sb", align_bytes=64)
-        ws_sb = keep.tile([P, G, H], U8, name="ws_sb", align_bytes=64)
+        xs_sb = keep.tile([P, N], U8, name="xs_sb", align_bytes=256)
+        ws_sb = keep.tile([P, G, H], U8, name="ws_sb", align_bytes=256)
+        zero = keep.tile([P, 512], BF16, name="zero")
+        nc.vector.memset(zero[:].bitcast(I32), 0)
         nc.vector.memset(xs_sb[:].bitcast(I32), 0)
         nc.vector.memset(ws_sb[:].rearrange("p g h -> p (g h)").bitcast(I32), 0)
 
@@ -53,21 +55,25 @@ def tile_skeleton_residual_contrasts_s3_kernel(tc, u, v_bytes, v_scale, c, x_wor
         v_raw, u_raw, c_raw = {}, {}, {}
 
         def load_v(j, g):
-            v_raw[j, g] = keep.tile([P, T4, WIDTHS[j]], U8, name="v_raw_%d_%d" % (j, g), align_bytes=64)
-            nc.sync.dma_start(out=v_raw[j, g][:], in_=v_rows[g][:, :, starts[j] : starts[j] + WIDTHS[j]])
+            width = WIDTHS[j] if j < 2 else 2 * WIDTHS[j]
+            raw = keep.tile([P, T4, width], U8, name="v_raw_%d_%d" % (j, g), align_bytes=64)
+            nc.sync.dma_start(out=raw[:], in_=v_rows[g][:, :, starts[j] : starts[j] + width])
+            v_raw[j, g] = raw[:, :, : WIDTHS[j]]
+            if j == 2:
+                v_raw[3, g] = raw[:, :, WIDTHS[j] :]
 
-        def load_u(a, i):
-            g, t = a // 2, 2 * (a % 2) + i
-            u_raw[a, i] = keep.tile([P, K], BF16, name="u_raw_%d_%d" % (a, i), align_bytes=64)
-            nc.sync.dma_start(out=u_raw[a, i][:], in_=u_rows[g][:, t, :])
+        def load_u(a):
+            g, t0 = a // 2, 2 * (a % 2)
+            u_raw[a] = keep.tile([P, 2, K], BF16, name="u_raw_%d" % a, align_bytes=64)
+            nc.sync.dma_start(out=u_raw[a][:], in_=u_rows[g][:, t0 : t0 + 2, :])
 
         def load_c(a):
             g, t0 = a // 2, 2 * (a % 2)
             c_raw[a] = keep.tile([P, 2, S], BF16, name="c_raw_%d" % a, align_bytes=64)
             nc.sync.dma_start(out=c_raw[a][:], in_=c_rows[g][:, t0 : t0 + 2, :])
 
-        x_sb = keep.tile([P, 2 * N], U8, name="x_sb", align_bytes=64)
-        w_sb = keep.tile([P, G, 2 * H], U8, name="w_sb", align_bytes=64)
+        x_sb = keep.tile([P, 2 * N], U8, name="x_sb", align_bytes=256)
+        w_sb = keep.tile([P, G, 2 * H], U8, name="w_sb", align_bytes=256)
 
         def load_x(lo, hi):
             nc.sync.dma_start(out=x_sb[:, lo:hi].bitcast(I32), in_=x_words[0][:, lo:hi].bitcast(I32))
@@ -84,12 +90,12 @@ def tile_skeleton_residual_contrasts_s3_kernel(tc, u, v_bytes, v_scale, c, x_wor
                 )
             nc.sync.dma_start(out=w_sb[:], in_=w_words.rearrange("g p n -> p g n"))
 
-        Q = {"headlen":1.64,"tr":1169,"cp":847,"qu":335,"qc":363,"tr_a":101,"sq":121,"q0":1136,"q01":930,"wS":1773,"wgS":473,"wtS":125,"wV":1445,"wgV":325,"wtV":105,"iv":1065,"ivg":489,"qv":797,"qvg":335,"ie":607,"qe":810,"ct":1305,"ctq":125,"st":167,"wide":["SSSV","SSSS","VVVV","SSSS","VSSV","SSVV"],"vt":["VS","SV","SS","VS"],"last":["B2","B2","S","S"],"loads":["xs","v00","v01","u00","u01","c0","u10","u11","c1","u20","u21","c2","x0","v10","u30","u31","c3","v11","v21","v30","v20","v31","x1","w"],"sp":-1324,"speng":["VSS","SVV","SVS","SSS"],"copyeng":["SSV","SSS","SSS","VVS"]}
+        Q = {"headlen":2512.03512,"tr":2615,"cp":-190,"qu":-3314,"qc":199,"tr_a":916,"sq":102,"q0":1743,"q01":4089,"wS":1143,"wgS":-110,"wtS":-599,"wV":1488,"wgV":533,"wtV":-93,"iv":908,"ivg":85,"qv":748,"qvg":50,"ie":588,"qe":906,"ct":1496,"ctq":130,"st":130,"wide":["SSSV","SSSS","VVVV","SSSS","VSSV","SSVV"],"vt":["VS","SV","SS","VS"],"last":["B2","B2","V","V"],"loads":["v00","u0","c0","v01","u1","c1","u2","xs","c2","x0","v10","u3","c3","v11","v20","x1","v21","w"],"sp":1128,"speng":["VSS","SVV","SVS","SSS"],"c0":14,"head":["k","w013","k","k","t00","w001","k","t01","w012","w002","w000","w003","t02","t11","t12","o01","o00","i00","w010","w011","o02","q00","u0","t10","i01","o12","o11","t20","t21","t22","c0","o20","q01","w102","w103","o10","r001","o21","r000","o22","c1","w100","t31","w101","s000","o31","t30","u1","s001","u2","t32","c2","r003","i10","w112","r010","w110","o32","o30","w113","r002","u3","c3","w111","r011","i11","s010","r013","s002","s003","s011","q10","r012","q11","s013","s012"],"style":[["PPPP","VVSS"],["SSVV","VSSV"],["VVSS","PPPP"],["SSSS","PPPP"]],"copyeng":["VSS","SSS","SVS","SSS"]}
         for name in Q["loads"]:
             if name[0] == "v":
                 load_v(int(name[1]), int(name[2]))
             elif name[0] == "u":
-                load_u(int(name[1]), int(name[2]))
+                load_u(int(name[1]))
             elif name[0] == "c":
                 load_c(int(name[1]))
             elif name == "xs":
@@ -104,9 +110,7 @@ def tile_skeleton_residual_contrasts_s3_kernel(tc, u, v_bytes, v_scale, c, x_wor
         warm = keep.tile([P, 1], F32, name="warm")
         nc.gpsimd.memset(warm[:], 0.0)
         nc.scalar.activation(out=warm[:], in_=warm[:], func=ACT.Square)
-        zero = keep.tile([P, 512], BF16, name="zero")
-        nc.vector.memset(zero[:], 0.0)
-        warm_bank = psum.tile([P, 512], F32, tag="o", bufs=3, name="warm_bank")
+        warm_bank = psum.tile([P, 512], F32, tag="o", bufs=2, name="warm_bank")
         for x in range(N_WARM):
             nc.tensor.matmul(warm_bank[:], lhsT=zero[:, :P], rhs=zero[:], start=True, stop=True)
         ident = keep.tile([P, P], F32, name="ident")
@@ -119,21 +123,18 @@ def tile_skeleton_residual_contrasts_s3_kernel(tc, u, v_bytes, v_scale, c, x_wor
         u_codes, u_scl, c_codes, c_scl = {}, {}, {}, {}
         banks = {}
 
-        def transposes_u(a, i):
-            words = u_raw[a, i][:].bitcast(F32)
-            bank = psum.tile([P, 4, P], F32, tag="r", bufs=5, name="ub")
-            for g in range(2):
-                for h in range(2):
-                    nc.tensor.transpose(bank[:, 2 * g + h, :], words[:, 256 * g + h : 256 * (g + 1) : 2], ident[:])
+        def transposes(a, i):
+            bank = psum.tile([P, 4, P], F32, tag="r", bufs=6, name="tb")
+            for b in range(4):
+                if i < 2:
+                    words = u_raw[a][:, i, :].bitcast(F32)[:, 256 * (b // 2) + b % 2 : 256 * (b // 2 + 1) : 2]
+                else:
+                    words = c_raw[a][:, b // 2, :].bitcast(F32)[:, b % 2 : 256 : 2]
+                nc.tensor.transpose(bank[:, b, :], words, ident[:])
             banks[a, i] = bank
 
-        def transposes_c(a):
-            bank = psum.tile([P, 4, P], F32, tag="r", bufs=5, name="cb")
-            for i in range(2):
-                words = c_raw[a][:, i, :].bitcast(F32)
-                for h in range(2):
-                    nc.tensor.transpose(bank[:, 2 * i + h, :], words[:, h:256:2], ident[:])
-            banks[a, 2] = bank
+        def keep_warm():
+            nc.tensor.matmul(warm_bank[:], lhsT=zero[:, :P], rhs=zero[:], start=True, stop=True)
 
         groups = {}
 
@@ -154,39 +155,42 @@ def tile_skeleton_residual_contrasts_s3_kernel(tc, u, v_bytes, v_scale, c, x_wor
 
         def quantize_u(a):
             gu = groups["u", a]
-            u_codes[a] = keep.tile([P, 512], U32, name="u_codes_%d" % a, align_bytes=64)
-            u_scl[a] = keep.tile([P, 512], U8, name="u_scl_%d" % a, align_bytes=64)
+            u_codes[a] = keep.tile([P, 512], U32, name="u_codes_%d" % a, align_bytes=256)
+            u_scl[a] = keep.tile([P, 512], U8, name="u_scl_%d" % a, align_bytes=256)
             nc.vector.quantize_mx(out=u_codes[a][:].bitcast(E4M3X4), scales=u_scl[a][:], in_=gu[:].rearrange("p i k -> p (i k)"))
 
         def quantize_c(a):
             gc = groups["c", a]
-            c_codes[a] = keep.tile([P, 256], U32, name="c_codes_%d" % a, align_bytes=64)
-            c_scl[a] = keep.tile([P, 256], U8, name="c_scl_%d" % a, align_bytes=64)
+            c_codes[a] = keep.tile([P, 256], U32, name="c_codes_%d" % a, align_bytes=256)
+            c_scl[a] = keep.tile([P, 256], U8, name="c_scl_%d" % a, align_bytes=256)
             nc.vector.quantize_mx(out=c_codes[a][:].bitcast(E4M3X4), scales=c_scl[a][:], in_=gc[:])
 
         v_wide, v_grp, v_codes, v_scl = {}, {}, {}, {}
 
-        def widen(j, g, t, engine):
+        def widen(j, g, t):
+            style = Q["style"][j][g]
             if (j, g) not in v_wide:
                 v_wide[j, g] = work.tile([P, T4 * WIDTHS[j]], BF16, tag="v_wide", bufs=5, name="v_wide", align_bytes=64)
             src = v_raw[j, g][:, t, :].bitcast(E4M3)
-            if engine == "S":
+            if style == "PPPP":
+                dst = v_wide[j, g][:].rearrange("p (r n e) -> p r n e", r=2, e=2)[:, t // 2, :, t % 2]
+            else:
                 dst = v_wide[j, g][:].rearrange("p (t n) -> p t n", t=T4)[:, t, :]
+            if style[t] == "S":
                 nc.scalar.activation(out=dst, in_=src, func=ACT.Copy, scale=vs_sb[:, g, t : t + 1])
             else:
-                dst = v_wide[j, g][:].rearrange("p (r n e) -> p r n e", r=2, e=2)[:, t // 2, :, t % 2]
                 nc.vector.tensor_scalar(out=dst, in0=src, scalar1=vs_sb[:, g, t : t + 1], scalar2=None, op0=ALU.mult)
 
         def interleave_v(j, g):
             v_grp[j, g] = work.tile([P, T4 * WIDTHS[j]], BF16, tag="v_grp", bufs=3, name="v_grp", align_bytes=64)
-            if Q["vt"][j][g] == "S":
-                nc.vector.tensor_copy(out=v_grp[j, g][:].rearrange("p (n t) -> p n t", t=T4), in_=v_wide[j, g][:].rearrange("p (t n) -> p n t", t=T4))
+            if Q["style"][j][g] != "PPPP":
+                nc.vector.tensor_copy(out=v_grp[j, g][:].rearrange("p (c i t) -> p c t i", i=4, t=T4), in_=v_wide[j, g][:].rearrange("p (t c i) -> p c t i", i=4, t=T4))
             else:
                 nc.vector.tensor_copy(out=v_grp[j, g][:].bitcast(F32).rearrange("p (n r) -> p n r", r=2), in_=v_wide[j, g][:].bitcast(F32).rearrange("p (r n) -> p n r", r=2))
 
         def quantize_v(j, g):
-            v_codes[j, g] = keep.tile([P, WIDTHS[j]], U32, name="v_codes_%d_%d" % (j, g), align_bytes=64)
-            v_scl[j, g] = keep.tile([P, WIDTHS[j]], U8, name="v_scl_%d_%d" % (j, g), align_bytes=64)
+            v_codes[j, g] = keep.tile([P, WIDTHS[j]], U32, name="v_codes_%d_%d" % (j, g), align_bytes=256)
+            v_scl[j, g] = keep.tile([P, WIDTHS[j]], U8, name="v_scl_%d_%d" % (j, g), align_bytes=256)
             nc.vector.quantize_mx(out=v_codes[j, g][:].bitcast(E4M3X4), scales=v_scl[j, g][:], in_=v_grp[j, g][:])
 
         r_banks, e_wide, e_grp, e_codes, e_scl = {}, {}, {}, {}, {}
@@ -194,7 +198,7 @@ def tile_skeleton_residual_contrasts_s3_kernel(tc, u, v_bytes, v_scale, c, x_wor
         def residual(j, g, t):
             a, i = 2 * g + t // 2, t % 2
             w = WIDTHS[j]
-            bank = psum.tile([P, w], F32, tag="r", bufs=5, name="rb")
+            bank = psum.tile([P, w], F32, tag="r", bufs=6, name="rb")
             r_banks[j, g, t] = bank
             cc = slice(P * i, P * i + P)
             step = w if w == 512 else P
@@ -218,25 +222,25 @@ def tile_skeleton_residual_contrasts_s3_kernel(tc, u, v_bytes, v_scale, c, x_wor
         def interleave_e(j, g, h):
             ew = WIDTHS[j] // PARTS[j]
             e_grp[j, g, h] = work.tile([P, ew, T4], BF16, tag="e_grp", bufs=3, name="e_grp", align_bytes=64)
-            nc.vector.tensor_copy(out=e_grp[j, g, h][:], in_=e_wide[j, g][:, :, h * ew : (h + 1) * ew].rearrange("p t n -> p n t"))
+            nc.vector.tensor_copy(out=e_grp[j, g, h][:].rearrange("p (c i) t -> p c t i", i=4), in_=e_wide[j, g][:, :, h * ew : (h + 1) * ew].rearrange("p t (c i) -> p c t i", i=4))
 
         def quantize_e(j, g, h):
             ew = WIDTHS[j] // PARTS[j]
-            e_codes[j, g, h] = work.tile([P, ew], U32, tag="e_codes", bufs=8, name="e_codes", align_bytes=64)
-            e_scl[j, g, h] = work.tile([P, ew], U8, tag="e_scl", bufs=8, name="e_scl", align_bytes=64)
+            e_codes[j, g, h] = work.tile([P, ew], U32, tag="e_codes", bufs=8, name="e_codes", align_bytes=256)
+            e_scl[j, g, h] = work.tile([P, ew], U8, tag="e_scl", bufs=8, name="e_scl", align_bytes=256)
             nc.vector.quantize_mx(out=e_codes[j, g, h][:].bitcast(E4M3X4), scales=e_scl[j, g, h][:], in_=e_grp[j, g, h][:].rearrange("p n t -> p (n t)"))
 
         o_banks = {}
 
-        def contrast(j, q):
-            bank = psum.tile([P, H], F32, tag="o", bufs=3, name="ob")
-            o_banks[j, q] = bank
+        def contrast(j, q, g):
+            if (j, q) not in o_banks:
+                tag = "r" if j == nj - 1 and q < 2 else "o"
+                o_banks[j, q] = psum.tile([P, H], F32, tag=tag, bufs=6 if tag == "r" else 2, name="ob")
             h, q0 = divmod(q, WIDTHS[j] // PARTS[j] // P)
             cq = slice(P * q0, P * q0 + P)
-            for g in range(G):
-                nc.tensor.matmul_mx(
-                    out=bank[:], lhsT=e_codes[j, g, h][:, cq].bitcast(E4M3X4), lhsT_scale=e_scl[j, g, h][:, cq],
-                    rhs=w_sb[:, g, :].bitcast(E2M1X4), rhs_scale=ws_sb[:, g, :], start=(g == 0), stop=(g == 1))
+            nc.tensor.matmul_mx(
+                out=o_banks[j, q][:], lhsT=e_codes[j, g, h][:, cq].bitcast(E4M3X4), lhsT_scale=e_scl[j, g, h][:, cq],
+                rhs=w_sb[:, g, :].bitcast(E2M1X4), rhs_scale=ws_sb[:, g, :], start=(g == 0), stop=(g == 1))
 
         def store(j, q, engine):
             r0 = starts[j] + P * q
@@ -257,40 +261,51 @@ def tile_skeleton_residual_contrasts_s3_kernel(tc, u, v_bytes, v_scale, c, x_wor
                         nc.vector.tensor_copy(out=o_half[:], in_=o_banks[j, q][:, cols])
                     nc.sync.dma_start(out=out[r0 : r0 + P, cols], in_=o_half[:])
 
-        lengths = [w * (Q["headlen"] if j == 0 else 1.0) for j, w in enumerate(WIDTHS)]
+        lengths = WIDTHS
         at = [2 * sum(lengths[:j]) for j in range(nj + 1)]
 
         def slot(j, g):
             return at[j] + g * lengths[j]
+
+        for name in Q["head"]:
+            n = [int(x) for x in name[1:]]
+            if name[0] == "t":
+                transposes(*n)
+            elif name[0] == "k":
+                keep_warm()
+            elif name[0] == "o":
+                copy_out(n[0], n[1], Q["copyeng"][n[0]][n[1]])
+            elif name[0] == "u":
+                quantize_u(*n)
+            elif name[0] == "c":
+                quantize_c(*n)
+            elif name[0] == "w":
+                widen(*n)
+            elif name[0] == "i":
+                interleave_v(*n)
+            elif name[0] == "q":
+                quantize_v(*n)
+            elif name[0] == "r":
+                residual(*n)
+            else:
+                square(*n)
 
         steps = []
 
         def add(key, fn, *args):
             steps.append((key, len(steps), fn, args))
 
-        for a in range(4):
-            base = slot(0, a // 2) + (a % 2) * lengths[0] / 2
-            for i in range(3):
-                add(base - Q["tr"] - Q["tr_a"] * (3 - a) + i, transposes_u if i < 2 else transposes_c, *((a, i) if i < 2 else (a,)))
-                e = Q["copyeng"][a][i]
-                add(base - Q["cp"] - Q["tr_a"] * (3 - a) + i, copy_out, a, i, e)
-            add(base - Q["qu"] - Q["tr_a"] * (3 - a), quantize_u, a)
-            add(base - Q["qc"] - Q["tr_a"] * (3 - a), quantize_c, a)
         for j in range(nj):
             for g in range(G):
                 for t in range(T4):
-                    key = slot(j, g) + t * lengths[j] / 4
-                    add(key, residual, j, g, t)
-                    add(key + Q["sq"], square, j, g, t)
-                    e = Q["vt"][j][g]
-                    if j == 0:
-                        add(at[0] - 3000 + 1000 * g + t, widen, j, g, t, e)
-                    else:
-                        add(at[j] - Q["w" + e] + g * Q["wg" + e] + t * Q["wt" + e], widen, j, g, t, e)
-                if j == 0:
-                    add(at[0] - 2500 + 1000 * g, interleave_v, j, g)
-                    add(at[0] - Q["q0"] + Q["q01"] * g, quantize_v, j, g)
-                else:
+                    if j > 0:
+                        key = slot(j, g) + t * lengths[j] / 4
+                        add(key, residual, j, g, t)
+                        add(key + Q["sq"], square, j, g, t)
+                    if j > 1:
+                        e = "V" if Q["style"][j][g][t] != "S" else "S"
+                        add(at[j] - Q["w" + e] + g * Q["wg" + e] + t * Q["wt" + e], widen, j, g, t)
+                if j > 1:
                     add(at[j] - Q["iv"] + g * Q["ivg"], interleave_v, j, g)
                     add(at[j] - Q["qv"] + g * Q["qvg"], quantize_v, j, g)
                 for h in range(PARTS[j]):
@@ -299,7 +314,8 @@ def tile_skeleton_residual_contrasts_s3_kernel(tc, u, v_bytes, v_scale, c, x_wor
                     add(slot(j, g + 1) + Q["qe"] + dh, quantize_e, j, g, h)
             for q in range(WIDTHS[j] // P):
                 key = at[j + 1] + Q["ct"] + q * Q["ctq"]
-                add(key, contrast, j, q)
+                add(key - (Q["c0"] if j == nj - 1 else 0), contrast, j, q, 0)
+                add(key + 0.5, contrast, j, q, 1)
                 add(key + Q["st"], store, j, q, "S" if j < nj - 1 else Q["last"][q])
         for key, n, fn, args in sorted(steps, key=lambda s: (s[0], s[1])):
             fn(*args)

@@ -18,304 +18,355 @@ ACT = mybir.ActivationFunctionType
 ALU = mybir.AluOpType
 
 P = 128
-T4 = 4
+PACK = 4
 G = 2
-WIDTHS = (512, 512, 512, 512)
-X_FIRST = 512
-N_WARM = 3
-PARTS = (1, 1, 1, 2)
+WIDTH = 512
+TILES = N // WIDTH
+PAIRS = 4
+WARM_UPS = 7
+
+WIDENERS = (("pairs", "SSSS"), ("pairs", "VSSS"), ("pairs", "VVSS"), ("SSVV", "SSVV"))
 
 
 def tile_skeleton_residual_contrasts_s3_kernel(tc, u, v_bytes, v_scale, c, x_words, x_scales, d, w_words, w_scales, out):
     nc = tc.nc
-    starts = [sum(WIDTHS[:j]) for j in range(len(WIDTHS))]
-    nj = len(WIDTHS)
 
     with ExitStack() as ctx:
         keep = ctx.enter_context(tc.tile_pool(name="keep", bufs=1))
-        work = ctx.enter_context(tc.tile_pool(name="work", bufs=3))
+        work = ctx.enter_context(tc.tile_pool(name="work", bufs=4))
         psum = ctx.enter_context(tc.psum_pool(name="psum", bufs=1))
         ctx.enter_context(tc.manual_schedule())
 
-        vs_sb = keep.tile([P, G, T4], F32, name="vs_sb")
-        nc.scalar.dma_start(out=vs_sb[:], in_=v_scale.rearrange("(g p t) o -> p g (t o)", p=P, t=T4))
-        d_sb = keep.tile([P, G, T4], BF16, name="d_sb")
-        nc.scalar.dma_start(out=d_sb[:], in_=d.rearrange("(g p t) -> p g t", p=P, t=T4))
+        def turn_bank(name):
+            return psum.tile([P, WIDTH], F32, tag="turn", bufs=6, name=name)
 
-        xs_sb = keep.tile([P, N], U8, name="xs_sb", align_bytes=256)
-        ws_sb = keep.tile([P, G, H], U8, name="ws_sb", align_bytes=256)
-        zero = keep.tile([P, 512], BF16, name="zero")
+        def out_bank(name):
+            return psum.tile([P, H], F32, tag="out", bufs=2, name=name)
+
+        vs_sb = keep.tile([P, G, PACK], F32, name="vs_sb")
+        nc.scalar.dma_start(out=vs_sb[:], in_=v_scale.rearrange("(g p t) o -> p g (t o)", p=P, t=PACK))
+        d_sb = keep.tile([P, G, PACK], BF16, name="d_sb")
+        nc.scalar.dma_start(out=d_sb[:], in_=d.rearrange("(g p t) -> p g t", p=P, t=PACK))
+
+        zero = keep.tile([P, WIDTH], BF16, name="zero")
         nc.vector.memset(zero[:].bitcast(I32), 0)
+        xs_sb = keep.tile([P, N], U8, name="xs_sb", align_bytes=256)
         nc.vector.memset(xs_sb[:].bitcast(I32), 0)
-        nc.vector.memset(ws_sb[:].rearrange("p g h -> p (g h)").bitcast(I32), 0)
-
-        v_rows = v_bytes.rearrange("(g p t) n -> g p t n", p=P, t=T4)
-        u_rows = u.rearrange("(g p t) k -> g p t k", p=P, t=T4)
-        c_rows = c.rearrange("(g p t) k -> g p t k", p=P, t=T4)
-        v_raw, u_raw, c_raw = {}, {}, {}
-
-        def load_v(j, g):
-            width = WIDTHS[j] if j < 2 else 2 * WIDTHS[j]
-            raw = keep.tile([P, T4, width], U8, name="v_raw_%d_%d" % (j, g), align_bytes=64)
-            nc.sync.dma_start(out=raw[:], in_=v_rows[g][:, :, starts[j] : starts[j] + width])
-            v_raw[j, g] = raw[:, :, : WIDTHS[j]]
-            if j == 2:
-                v_raw[3, g] = raw[:, :, WIDTHS[j] :]
-
-        def load_u(a):
-            g, t0 = a // 2, 2 * (a % 2)
-            u_raw[a] = keep.tile([P, 2, K], BF16, name="u_raw_%d" % a, align_bytes=64)
-            nc.sync.dma_start(out=u_raw[a][:], in_=u_rows[g][:, t0 : t0 + 2, :])
-
-        def load_c(a):
-            g, t0 = a // 2, 2 * (a % 2)
-            c_raw[a] = keep.tile([P, 2, S], BF16, name="c_raw_%d" % a, align_bytes=64)
-            nc.sync.dma_start(out=c_raw[a][:], in_=c_rows[g][:, t0 : t0 + 2, :])
-
+        ws_sb = keep.tile([P, G * H], U8, name="ws_sb", align_bytes=256)
+        nc.vector.memset(ws_sb[:].bitcast(I32), 0)
         x_sb = keep.tile([P, 2 * N], U8, name="x_sb", align_bytes=256)
         w_sb = keep.tile([P, G, 2 * H], U8, name="w_sb", align_bytes=256)
 
-        def load_x(lo, hi):
-            nc.sync.dma_start(out=x_sb[:, lo:hi].bitcast(I32), in_=x_words[0][:, lo:hi].bitcast(I32))
+        v_rows = v_bytes.rearrange("(g p t) n -> g p t n", p=P, t=PACK)
+        u_rows = u.rearrange("(g p t) k -> g p t k", p=P, t=PACK)
+        c_rows = c.rearrange("(g p t) k -> g p t k", p=P, t=PACK)
+        v_raw, u_raw, c_raw = {}, {}, {}
 
-        def load_xs():
-            for q in range(4):
-                nc.sync.dma_start(out=xs_sb[32 * q : 32 * q + 4, :].bitcast(I32), in_=x_scales[0][4 * q : 4 * q + 4, :].bitcast(I32))
+        def load_v(j, g, tiles=1):
+            raw = keep.tile([P, PACK, tiles * WIDTH], U8, name="v_raw_%d_%d" % (j, g), align_bytes=64)
+            nc.sync.dma_start(out=raw[:], in_=v_rows[g][:, :, j * WIDTH : (j + tiles) * WIDTH])
+            for n in range(tiles):
+                v_raw[j + n, g] = raw[:, :, n * WIDTH : (n + 1) * WIDTH]
 
-        def load_w():
-            for q in range(4):
-                nc.sync.dma_start(
-                    out=ws_sb[32 * q : 32 * q + 4, :, :].rearrange("q g h -> q (g h)").bitcast(I32).rearrange("q (g h) -> q g h", g=G),
-                    in_=w_scales.bitcast(I32).rearrange("g q h -> q g h")[4 * q : 4 * q + 4, :, :],
-                )
-            nc.sync.dma_start(out=w_sb[:], in_=w_words.rearrange("g p n -> p g n"))
+        def load_u(a):
+            u_raw[a] = keep.tile([P, 2, K], BF16, name="u_raw_%d" % a, align_bytes=64)
+            nc.sync.dma_start(out=u_raw[a][:], in_=u_rows[a // 2][:, 2 * (a % 2) : 2 * (a % 2) + 2, :])
 
-        Q = {"headlen":2512.03512,"tr":2615,"cp":-190,"qu":-3314,"qc":199,"tr_a":916,"sq":102,"q0":1743,"q01":4089,"wS":1143,"wgS":-110,"wtS":-599,"wV":1488,"wgV":533,"wtV":-93,"iv":908,"ivg":85,"qv":748,"qvg":50,"ie":588,"qe":906,"ct":1496,"ctq":130,"st":130,"wide":["SSSV","SSSS","VVVV","SSSS","VSSV","SSVV"],"vt":["VS","SV","SS","VS"],"last":["B2","B2","V","V"],"loads":["v00","u0","c0","v01","u1","c1","u2","xs","c2","x0","v10","u3","c3","v11","v20","x1","v21","w"],"sp":1128,"speng":["VSS","SVV","SVS","SSS"],"c0":14,"head":["k","w013","k","k","t00","w001","k","t01","w012","w002","w000","w003","t02","t11","t12","o01","o00","i00","w010","w011","o02","q00","u0","t10","i01","o12","o11","t20","t21","t22","c0","o20","q01","w102","w103","o10","r001","o21","r000","o22","c1","w100","t31","w101","s000","o31","t30","u1","s001","u2","t32","c2","r003","i10","w112","r010","w110","o32","o30","w113","r002","u3","c3","w111","r011","i11","s010","r013","s002","s003","s011","q10","r012","q11","s013","s012"],"style":[["PPPP","VVSS"],["SSVV","VSSV"],["VVSS","PPPP"],["SSSS","PPPP"]],"copyeng":["VSS","SSS","SVS","SSS"]}
-        for name in Q["loads"]:
-            if name[0] == "v":
-                load_v(int(name[1]), int(name[2]))
-            elif name[0] == "u":
-                load_u(int(name[1]))
-            elif name[0] == "c":
-                load_c(int(name[1]))
-            elif name == "xs":
-                load_xs()
-            elif name == "x0":
-                load_x(0, 2 * X_FIRST)
-            elif name == "x1":
-                load_x(2 * X_FIRST, 2 * N)
-            else:
-                load_w()
+        def load_c(a):
+            c_raw[a] = keep.tile([P, 2, S], BF16, name="c_raw_%d" % a, align_bytes=64)
+            nc.sync.dma_start(out=c_raw[a][:], in_=c_rows[a // 2][:, 2 * (a % 2) : 2 * (a % 2) + 2, :])
 
-        warm = keep.tile([P, 1], F32, name="warm")
-        nc.gpsimd.memset(warm[:], 0.0)
-        nc.scalar.activation(out=warm[:], in_=warm[:], func=ACT.Square)
-        warm_bank = psum.tile([P, 512], F32, tag="o", bufs=2, name="warm_bank")
-        for x in range(N_WARM):
-            nc.tensor.matmul(warm_bank[:], lhsT=zero[:, :P], rhs=zero[:], start=True, stop=True)
+        def load_x(first, last):
+            cols = slice(2 * WIDTH * first, 2 * WIDTH * last)
+            nc.sync.dma_start(out=x_sb[:, cols].bitcast(I32), in_=x_words[0][:, cols].bitcast(I32))
+
+        load_v(0, 0)
+        load_c(0)
+        load_v(0, 1)
+        load_u(0)
+        load_c(1)
+        for q in range(4):
+            nc.sync.dma_start(out=xs_sb[32 * q : 32 * q + 4, :].bitcast(I32), in_=x_scales[0][4 * q : 4 * q + 4, :].bitcast(I32))
+        load_x(0, 1)
+        load_u(1)
+        load_c(2)
+        load_v(1, 0)
+        load_c(3)
+        load_u(2)
+        load_u(3)
+        load_v(1, 1)
+        load_v(2, 0, tiles=2)
+        load_x(1, TILES)
+        load_v(2, 1, tiles=2)
+        for q in range(4):
+            nc.sync.dma_start(
+                out=ws_sb[32 * q : 32 * q + 4, :].bitcast(I32).rearrange("q (g h) -> q g h", g=G),
+                in_=w_scales.bitcast(I32).rearrange("g q h -> q g h")[4 * q : 4 * q + 4, :, :],
+            )
+        nc.sync.dma_start(out=w_sb[:], in_=w_words.rearrange("g p n -> p g n"))
+
+        table = keep.tile([P, 1], F32, name="table")
+        nc.gpsimd.memset(table[:], 0.0)
+        nc.scalar.activation(out=table[:], in_=table[:], func=ACT.Square)
+        warm = out_bank("warm")
+
+        def keep_warm(matmuls):
+            for n in range(matmuls):
+                nc.tensor.matmul(warm[:], lhsT=zero[:, :P], rhs=zero[:], start=True, stop=True)
+
+        keep_warm(WARM_UPS)
         ident = keep.tile([P, P], F32, name="ident")
         make_identity(nc, ident[:])
-        half = keep.tile([P, G, T4], F32, name="half")
+        half = keep.tile([P, G, PACK], F32, name="half")
         nc.gpsimd.memset(half[:], 0.5)
-        root = keep.tile([P, G, T4], F32, name="root")
+        root = keep.tile([P, G, PACK], F32, name="root")
         nc.gpsimd.tensor_tensor(out=root[:], in0=d_sb[:], in1=half[:], op=ALU.pow)
 
-        u_codes, u_scl, c_codes, c_scl = {}, {}, {}, {}
-        banks = {}
+        def quantize(name, grouped, words):
+            codes = keep.tile([P, words], U32, name=name, align_bytes=256)
+            scales = keep.tile([P, words], U8, name=name + "_scales", align_bytes=256)
+            nc.vector.quantize_mx(out=codes[:].bitcast(E4M3X4), scales=scales[:], in_=grouped)
+            return codes, scales
 
-        def transposes(a, i):
-            bank = psum.tile([P, 4, P], F32, tag="r", bufs=6, name="tb")
-            for b in range(4):
-                if i < 2:
-                    words = u_raw[a][:, i, :].bitcast(F32)[:, 256 * (b // 2) + b % 2 : 256 * (b // 2 + 1) : 2]
-                else:
-                    words = c_raw[a][:, b // 2, :].bitcast(F32)[:, b % 2 : 256 : 2]
-                nc.tensor.transpose(bank[:, b, :], words, ident[:])
-            banks[a, i] = bank
+        turned, u_grouped, c_grouped, u_mx, c_mx = {}, {}, {}, {}, {}
 
-        def keep_warm():
-            nc.tensor.matmul(warm_bank[:], lhsT=zero[:, :P], rhs=zero[:], start=True, stop=True)
+        def turn(name, a, views):
+            turned[name, a] = turn_bank("turned")[:].rearrange("p (b r) -> p b r", b=4)
+            for b, view in enumerate(views):
+                nc.tensor.transpose(turned[name, a][:, b, :], view, ident[:])
 
-        groups = {}
+        def turn_u(a, i):
+            words = u_raw[a][:, i, :].bitcast(F32)
+            turn("u%d" % i, a, [words[:, 256 * g + e : 256 * (g + 1) : 2] for g in range(G) for e in range(2)])
 
-        def copy_out(a, i, engine):
-            if i < 2:
-                if ("u", a) not in groups:
-                    groups["u", a] = work.tile([P, 2, 1024], BF16, tag="gu", bufs=3, name="gu", align_bytes=64)
-                dst = groups["u", a][:, i, :]
-            else:
-                groups["c", a] = work.tile([P, 1024], BF16, tag="gc", bufs=3, name="gc", align_bytes=64)
-                dst = groups["c", a][:]
-            dst = dst.bitcast(F32).rearrange("p (g r h) -> p g r h", g=2, h=2)
-            src = banks[a, i][:].rearrange("p (g h) r -> p g r h", g=2)
-            if engine == "S":
-                nc.scalar.copy(out=dst, in_=src)
-            else:
-                nc.vector.tensor_copy(out=dst, in_=src)
+        def turn_c(a):
+            turn("c", a, [c_raw[a][:, i, :].bitcast(F32)[:, e:256:2] for i in range(2) for e in range(2)])
+
+        def collect(copy, name, a, dst):
+            copy(
+                out=dst.bitcast(F32).rearrange("p (b r e) -> p b r e", b=2, e=2),
+                in_=turned[name, a].rearrange("p (b e) r -> p b r e", b=2),
+            )
+
+        def collect_u(copy, a, i):
+            if i == 0:
+                u_grouped[a] = work.tile([P, 2 * 2 * P * PACK], BF16, tag="u_grouped", bufs=3, name="u_grouped", align_bytes=64)
+            collect(copy, "u%d" % i, a, u_grouped[a][:, 2 * P * PACK * i : 2 * P * PACK * (i + 1)])
+
+        def collect_c(copy, a):
+            c_grouped[a] = work.tile([P, 2 * P * PACK], BF16, tag="c_grouped", bufs=3, name="c_grouped", align_bytes=64)
+            collect(copy, "c", a, c_grouped[a][:])
 
         def quantize_u(a):
-            gu = groups["u", a]
-            u_codes[a] = keep.tile([P, 512], U32, name="u_codes_%d" % a, align_bytes=256)
-            u_scl[a] = keep.tile([P, 512], U8, name="u_scl_%d" % a, align_bytes=256)
-            nc.vector.quantize_mx(out=u_codes[a][:].bitcast(E4M3X4), scales=u_scl[a][:], in_=gu[:].rearrange("p i k -> p (i k)"))
+            u_mx[a] = quantize("u_codes_%d" % a, u_grouped[a][:], 2 * G * P)
 
         def quantize_c(a):
-            gc = groups["c", a]
-            c_codes[a] = keep.tile([P, 256], U32, name="c_codes_%d" % a, align_bytes=256)
-            c_scl[a] = keep.tile([P, 256], U8, name="c_scl_%d" % a, align_bytes=256)
-            nc.vector.quantize_mx(out=c_codes[a][:].bitcast(E4M3X4), scales=c_scl[a][:], in_=gc[:])
+            c_mx[a] = quantize("c_codes_%d" % a, c_grouped[a][:], 2 * P)
 
-        v_wide, v_grp, v_codes, v_scl = {}, {}, {}, {}
+        v_wide, v_grouped, v_mx = {}, {}, {}
 
-        def widen(j, g, t):
-            style = Q["style"][j][g]
+        def widen(j, g, planes=range(PACK)):
+            way = WIDENERS[j][g]
             if (j, g) not in v_wide:
-                v_wide[j, g] = work.tile([P, T4 * WIDTHS[j]], BF16, tag="v_wide", bufs=5, name="v_wide", align_bytes=64)
-            src = v_raw[j, g][:, t, :].bitcast(E4M3)
-            if style == "PPPP":
-                dst = v_wide[j, g][:].rearrange("p (r n e) -> p r n e", r=2, e=2)[:, t // 2, :, t % 2]
-            else:
-                dst = v_wide[j, g][:].rearrange("p (t n) -> p t n", t=T4)[:, t, :]
-            if style[t] == "S":
-                nc.scalar.activation(out=dst, in_=src, func=ACT.Copy, scale=vs_sb[:, g, t : t + 1])
-            else:
-                nc.vector.tensor_scalar(out=dst, in0=src, scalar1=vs_sb[:, g, t : t + 1], scalar2=None, op0=ALU.mult)
+                v_wide[j, g] = work.tile([P, PACK * WIDTH], BF16, tag="v_wide", bufs=5, name="v_wide", align_bytes=64)
+            for s in planes:
+                src = v_raw[j, g][:, s, :].bitcast(E4M3)
+                scale = vs_sb[:, g, s : s + 1]
+                if way == "pairs":
+                    dst = v_wide[j, g][:].rearrange("p (r n e) -> p r n e", r=2, e=2)[:, s // 2, :, s % 2]
+                else:
+                    dst = v_wide[j, g][:].rearrange("p (s n) -> p s n", s=PACK)[:, s, :]
+                if way[s] == "S":
+                    nc.scalar.activation(out=dst, in_=src, func=ACT.Copy, scale=scale)
+                else:
+                    nc.vector.tensor_scalar(out=dst, in0=src, scalar1=scale, scalar2=None, op0=ALU.mult)
+
+        def widen_on(engine, j, g):
+            way = WIDENERS[j][g]
+            widen(j, g, [s for s in range(PACK) if (engine == "V" if way == "pairs" else way[s] == engine)])
 
         def interleave_v(j, g):
-            v_grp[j, g] = work.tile([P, T4 * WIDTHS[j]], BF16, tag="v_grp", bufs=3, name="v_grp", align_bytes=64)
-            if Q["style"][j][g] != "PPPP":
-                nc.vector.tensor_copy(out=v_grp[j, g][:].rearrange("p (c i t) -> p c t i", i=4, t=T4), in_=v_wide[j, g][:].rearrange("p (t c i) -> p c t i", i=4, t=T4))
+            v_grouped[j, g] = work.tile([P, PACK * WIDTH], BF16, tag="v_grouped", bufs=3, name="v_grouped", align_bytes=64)
+            dst, src = v_grouped[j, g][:], v_wide[j, g][:]
+            if WIDENERS[j][g] == "pairs":
+                nc.vector.tensor_copy(
+                    out=dst.bitcast(F32).rearrange("p (n r) -> p n r", r=2),
+                    in_=src.bitcast(F32).rearrange("p (r n) -> p n r", r=2),
+                )
             else:
-                nc.vector.tensor_copy(out=v_grp[j, g][:].bitcast(F32).rearrange("p (n r) -> p n r", r=2), in_=v_wide[j, g][:].bitcast(F32).rearrange("p (r n) -> p n r", r=2))
+                nc.vector.tensor_copy(
+                    out=dst.rearrange("p (c i s) -> p c s i", i=4, s=PACK),
+                    in_=src.rearrange("p (s c i) -> p c s i", i=4, s=PACK),
+                )
 
         def quantize_v(j, g):
-            v_codes[j, g] = keep.tile([P, WIDTHS[j]], U32, name="v_codes_%d_%d" % (j, g), align_bytes=256)
-            v_scl[j, g] = keep.tile([P, WIDTHS[j]], U8, name="v_scl_%d_%d" % (j, g), align_bytes=256)
-            nc.vector.quantize_mx(out=v_codes[j, g][:].bitcast(E4M3X4), scales=v_scl[j, g][:], in_=v_grp[j, g][:])
+            v_mx[j, g] = quantize("v_codes_%d_%d" % (j, g), v_grouped[j, g][:], WIDTH)
 
-        r_banks, e_wide, e_grp, e_codes, e_scl = {}, {}, {}, {}, {}
+        r_banks = {}
 
-        def residual(j, g, t):
-            a, i = 2 * g + t // 2, t % 2
-            w = WIDTHS[j]
-            bank = psum.tile([P, w], F32, tag="r", bufs=6, name="rb")
-            r_banks[j, g, t] = bank
-            cc = slice(P * i, P * i + P)
-            step = w if w == 512 else P
-            for n in range(0, w, step):
-                nn = slice(n, n + step)
-                n0 = starts[j] + n
+        def residual_cx(j, g, t):
+            r_banks[j, g, t] = turn_bank("residual")
+            codes, scales = c_mx[2 * g + t // 2]
+            rows = slice(P * (t % 2), P * (t % 2 + 1))
+            nc.tensor.matmul_mx(
+                out=r_banks[j, g, t][:],
+                lhsT=codes[:, rows].bitcast(E4M3X4),
+                lhsT_scale=scales[:, rows],
+                rhs=x_sb[:, 2 * WIDTH * j : 2 * WIDTH * (j + 1)].bitcast(E2M1X4),
+                rhs_scale=xs_sb[:, WIDTH * j : WIDTH * (j + 1)],
+                start=True,
+                stop=False,
+            )
+
+        def residual_uv(j, g, t):
+            codes, scales = u_mx[2 * g + t // 2]
+            for k in range(G):
+                rows = slice(P * (G * (t % 2) + k), P * (G * (t % 2) + k + 1))
+                v_codes, v_scales = v_mx[j, k]
                 nc.tensor.matmul_mx(
-                    out=bank[:, nn], lhsT=c_codes[a][:, cc].bitcast(E4M3X4), lhsT_scale=c_scl[a][:, cc],
-                    rhs=x_sb[:, 2 * n0 : 2 * (n0 + step)].bitcast(E2M1X4), rhs_scale=xs_sb[:, n0 : n0 + step], start=True, stop=False)
-                for k in range(2):
-                    cu = slice(256 * i + P * k, 256 * i + P * k + P)
-                    nc.tensor.matmul_mx(
-                        out=bank[:, nn], lhsT=u_codes[a][:, cu].bitcast(E4M3X4), lhsT_scale=u_scl[a][:, cu],
-                        rhs=v_codes[j, k][:, nn].bitcast(E4M3X4), rhs_scale=v_scl[j, k][:, nn], start=False, stop=(k == 1))
+                    out=r_banks[j, g, t][:],
+                    lhsT=codes[:, rows].bitcast(E4M3X4),
+                    lhsT_scale=scales[:, rows],
+                    rhs=v_codes[:].bitcast(E4M3X4),
+                    rhs_scale=v_scales[:],
+                    start=False,
+                    stop=(k == G - 1),
+                )
+
+        e_wide, e_grouped, e_mx = {}, {}, {}
 
         def square(j, g, t):
             if (j, g) not in e_wide:
-                e_wide[j, g] = work.tile([P, T4, WIDTHS[j]], BF16, tag="e_wide", bufs=4, name="e_wide", align_bytes=64)
+                e_wide[j, g] = work.tile([P, PACK, WIDTH], BF16, tag="e_wide", bufs=4, name="e_wide", align_bytes=64)
             nc.scalar.activation(out=e_wide[j, g][:, t, :], in_=r_banks[j, g, t][:], func=ACT.Square, scale=root[:, g, t : t + 1])
 
-        def interleave_e(j, g, h):
-            ew = WIDTHS[j] // PARTS[j]
-            e_grp[j, g, h] = work.tile([P, ew, T4], BF16, tag="e_grp", bufs=3, name="e_grp", align_bytes=64)
-            nc.vector.tensor_copy(out=e_grp[j, g, h][:].rearrange("p (c i) t -> p c t i", i=4), in_=e_wide[j, g][:, :, h * ew : (h + 1) * ew].rearrange("p t (c i) -> p c t i", i=4))
+        def halves(j):
+            return 2 if j == TILES - 1 else 1
 
-        def quantize_e(j, g, h):
-            ew = WIDTHS[j] // PARTS[j]
-            e_codes[j, g, h] = work.tile([P, ew], U32, tag="e_codes", bufs=8, name="e_codes", align_bytes=256)
-            e_scl[j, g, h] = work.tile([P, ew], U8, tag="e_scl", bufs=8, name="e_scl", align_bytes=256)
-            nc.vector.quantize_mx(out=e_codes[j, g, h][:].bitcast(E4M3X4), scales=e_scl[j, g, h][:], in_=e_grp[j, g, h][:].rearrange("p n t -> p (n t)"))
+        def interleave_e(j, g, part=0):
+            cols = WIDTH // halves(j)
+            e_grouped[j, g, part] = work.tile([P, cols * PACK], BF16, tag="e_grouped", bufs=3, name="e_grouped", align_bytes=64)
+            nc.vector.tensor_copy(
+                out=e_grouped[j, g, part][:].rearrange("p (c i t) -> p c t i", i=4, t=PACK),
+                in_=e_wide[j, g][:, :, part * cols : (part + 1) * cols].rearrange("p t (c i) -> p c t i", i=4),
+            )
+
+        def quantize_e(j, g, part=0):
+            e_mx[j, g, part] = quantize("e_codes_%d_%d_%d" % (j, g, part), e_grouped[j, g, part][:], WIDTH // halves(j))
 
         o_banks = {}
 
-        def contrast(j, q, g):
-            if (j, q) not in o_banks:
-                tag = "r" if j == nj - 1 and q < 2 else "o"
-                o_banks[j, q] = psum.tile([P, H], F32, tag=tag, bufs=6 if tag == "r" else 2, name="ob")
-            h, q0 = divmod(q, WIDTHS[j] // PARTS[j] // P)
-            cq = slice(P * q0, P * q0 + P)
-            nc.tensor.matmul_mx(
-                out=o_banks[j, q][:], lhsT=e_codes[j, g, h][:, cq].bitcast(E4M3X4), lhsT_scale=e_scl[j, g, h][:, cq],
-                rhs=w_sb[:, g, :].bitcast(E2M1X4), rhs_scale=ws_sb[:, g, :], start=(g == 0), stop=(g == 1))
-
-        def store(j, q, engine):
-            r0 = starts[j] + P * q
-            if len(engine) == 1:
-                o_sb = work.tile([P, H], F32, tag="o_sb", bufs=4, name="o_sb", align_bytes=64)
-                if engine == "S":
-                    nc.scalar.copy(out=o_sb[:], in_=o_banks[j, q][:])
-                else:
-                    nc.vector.tensor_copy(out=o_sb[:], in_=o_banks[j, q][:])
-                nc.sync.dma_start(out=out[r0 : r0 + P, :], in_=o_sb[:])
-            else:
-                for h in range(2):
-                    o_half = work.tile([P, H // 2], F32, tag="o_half", bufs=4, name="o_half", align_bytes=64)
-                    cols = slice(h * H // 2, (h + 1) * H // 2)
-                    if h == 0:
-                        nc.scalar.copy(out=o_half[:], in_=o_banks[j, q][:, cols])
-                    else:
-                        nc.vector.tensor_copy(out=o_half[:], in_=o_banks[j, q][:, cols])
-                    nc.sync.dma_start(out=out[r0 : r0 + P, cols], in_=o_half[:])
-
-        lengths = WIDTHS
-        at = [2 * sum(lengths[:j]) for j in range(nj + 1)]
-
-        def slot(j, g):
-            return at[j] + g * lengths[j]
-
-        for name in Q["head"]:
-            n = [int(x) for x in name[1:]]
-            if name[0] == "t":
-                transposes(*n)
-            elif name[0] == "k":
-                keep_warm()
-            elif name[0] == "o":
-                copy_out(n[0], n[1], Q["copyeng"][n[0]][n[1]])
-            elif name[0] == "u":
-                quantize_u(*n)
-            elif name[0] == "c":
-                quantize_c(*n)
-            elif name[0] == "w":
-                widen(*n)
-            elif name[0] == "i":
-                interleave_v(*n)
-            elif name[0] == "q":
-                quantize_v(*n)
-            elif name[0] == "r":
-                residual(*n)
-            else:
-                square(*n)
-
-        steps = []
-
-        def add(key, fn, *args):
-            steps.append((key, len(steps), fn, args))
-
-        for j in range(nj):
+        def contrast(j, q):
+            o_banks[j, q] = out_bank("contrasts")
+            part, n = divmod(q, WIDTH // halves(j) // P)
             for g in range(G):
-                for t in range(T4):
-                    if j > 0:
-                        key = slot(j, g) + t * lengths[j] / 4
-                        add(key, residual, j, g, t)
-                        add(key + Q["sq"], square, j, g, t)
-                    if j > 1:
-                        e = "V" if Q["style"][j][g][t] != "S" else "S"
-                        add(at[j] - Q["w" + e] + g * Q["wg" + e] + t * Q["wt" + e], widen, j, g, t)
-                if j > 1:
-                    add(at[j] - Q["iv"] + g * Q["ivg"], interleave_v, j, g)
-                    add(at[j] - Q["qv"] + g * Q["qvg"], quantize_v, j, g)
-                for h in range(PARTS[j]):
-                    dh = h * lengths[j] / PARTS[j]
-                    add(slot(j, g + 1) + Q["ie"] + dh, interleave_e, j, g, h)
-                    add(slot(j, g + 1) + Q["qe"] + dh, quantize_e, j, g, h)
-            for q in range(WIDTHS[j] // P):
-                key = at[j + 1] + Q["ct"] + q * Q["ctq"]
-                add(key - (Q["c0"] if j == nj - 1 else 0), contrast, j, q, 0)
-                add(key + 0.5, contrast, j, q, 1)
-                add(key + Q["st"], store, j, q, "S" if j < nj - 1 else Q["last"][q])
-        for key, n, fn, args in sorted(steps, key=lambda s: (s[0], s[1])):
-            fn(*args)
+                codes, scales = e_mx[j, g, part]
+                nc.tensor.matmul_mx(
+                    out=o_banks[j, q][:],
+                    lhsT=codes[:, P * n : P * (n + 1)].bitcast(E4M3X4),
+                    lhsT_scale=scales[:, P * n : P * (n + 1)],
+                    rhs=w_sb[:, g, :].bitcast(E2M1X4),
+                    rhs_scale=ws_sb[:, H * g : H * (g + 1)],
+                    start=(g == 0),
+                    stop=(g == G - 1),
+                )
+
+        def store(j, q, copy):
+            o_sb = work.tile([P, H], F32, tag="o_sb", bufs=6, name="o_sb", align_bytes=64)
+            copy(out=o_sb[:], in_=o_banks[j, q][:])
+            row = WIDTH * j + P * q
+            nc.sync.dma_start(out=out[row : row + P, :], in_=o_sb[:])
+
+        by_scalar, by_vector = nc.scalar.copy, nc.vector.tensor_copy
+
+        widen(0, 1)
+        widen(0, 0, range(0, 3))
+        turn_c(0)
+        collect_c(by_vector, 0)
+        widen(0, 0, range(3, 4))
+        keep_warm(2)
+        turn_u(0, 0)
+        turn_u(0, 1)
+        collect_u(by_scalar, 0, 0)
+        collect_u(by_scalar, 0, 1)
+        quantize_c(0)
+        interleave_v(0, 0)
+        interleave_v(0, 1)
+        turn_c(1)
+        collect_c(by_scalar, 1)
+        residual_cx(0, 0, 0)
+        residual_cx(0, 0, 1)
+        turn_u(1, 0)
+        collect_u(by_scalar, 1, 0)
+        turn_c(2)
+        collect_c(by_scalar, 2)
+        turn_u(1, 1)
+        collect_u(by_scalar, 1, 1)
+        quantize_u(0)
+        quantize_v(0, 0)
+        quantize_v(0, 1)
+        widen(1, 0)
+        for t in range(2):
+            residual_uv(0, 0, t)
+            square(0, 0, t)
+        quantize_u(1)
+        quantize_c(1)
+        turn_c(3)
+        collect_c(by_vector, 3)
+        for a in (2, 3):
+            for i in range(2):
+                turn_u(a, i)
+                collect_u(by_scalar, a, i)
+        widen(1, 1)
+        quantize_c(2)
+        quantize_u(2)
+        quantize_c(3)
+        interleave_v(1, 0)
+        quantize_u(3)
+        interleave_v(1, 1)
+        for g, t in ((0, 2), (0, 3), (1, 0), (1, 1), (1, 2), (1, 3)):
+            residual_cx(0, g, t)
+            residual_uv(0, g, t)
+            square(0, g, t)
+        for g in range(G):
+            quantize_v(1, g)
+
+        for g in range(G):
+            widen(2, g)
+        for j in range(1, TILES):
+            if j == 1:
+                for g in range(G):
+                    widen_on("S", 3, g)
+            for g in range(G):
+                for t in range(PACK):
+                    if g == 1 and j >= 2:
+                        contrast(j - 2, t)
+                        store(j - 2, t, by_scalar)
+                    residual_cx(j, g, t)
+                    residual_uv(j, g, t)
+                    square(j, g, t)
+            if j + 1 < TILES:
+                interleave_v(j + 1, 0)
+                interleave_v(j + 1, 1)
+            interleave_e(j - 1, 0)
+            if j + 1 < TILES:
+                quantize_v(j + 1, 0)
+                quantize_v(j + 1, 1)
+            quantize_e(j - 1, 0)
+            interleave_e(j - 1, 1)
+            if j == 1:
+                for g in range(G):
+                    widen_on("V", 3, g)
+            quantize_e(j - 1, 1)
+
+        last = TILES - 1
+        for q in range(WIDTH // P):
+            contrast(last - 1, q)
+            store(last - 1, q, by_scalar)
+        for g in range(G):
+            for part in range(2):
+                interleave_e(last, g, part)
+                quantize_e(last, g, part)
+        for q in range(WIDTH // P):
+            contrast(last, q)
+            store(last, q, [by_scalar, by_vector][q % 2])

from contextlib import ExitStack

import concourse.mybir as mybir
from concourse.masks import make_identity

M, N, K, S, H = 1024, 2048, 1024, 512, 512
FLOPS = 2 * M * N * (K + S) + 2 * N * M * H

F32 = mybir.dt.float32
BF16 = mybir.dt.bfloat16
I32 = mybir.dt.int32
U32 = mybir.dt.uint32
U8 = mybir.dt.uint8
E4M3 = mybir.dt.float8_e4m3fn
E4M3X4 = mybir.dt.float8_e4m3fn_x4
E2M1X4 = mybir.dt.float4_e2m1fn_x4
ACT = mybir.ActivationFunctionType
ALU = mybir.AluOpType

P = 128
PACK = 4
G = 2
WIDTH = 512
TILES = N // WIDTH
PAIRS = 4
WARM_UPS = 7

WIDENERS = (("pairs", "SSSS"), ("pairs", "VSSS"), ("pairs", "VVSS"), ("SSVV", "SSVV"))


def tile_skeleton_residual_contrasts_s3_kernel(tc, u, v_bytes, v_scale, c, x_words, x_scales, d, w_words, w_scales, out):
    nc = tc.nc

    with ExitStack() as ctx:
        keep = ctx.enter_context(tc.tile_pool(name="keep", bufs=1))
        work = ctx.enter_context(tc.tile_pool(name="work", bufs=4))
        psum = ctx.enter_context(tc.psum_pool(name="psum", bufs=1))
        ctx.enter_context(tc.manual_schedule())

        def turn_bank(name):
            return psum.tile([P, WIDTH], F32, tag="turn", bufs=6, name=name)

        def out_bank(name):
            return psum.tile([P, H], F32, tag="out", bufs=2, name=name)

        vs_sb = keep.tile([P, G, PACK], F32, name="vs_sb")
        nc.scalar.dma_start(out=vs_sb[:], in_=v_scale.rearrange("(g p t) o -> p g (t o)", p=P, t=PACK))
        d_sb = keep.tile([P, G, PACK], BF16, name="d_sb")
        nc.scalar.dma_start(out=d_sb[:], in_=d.rearrange("(g p t) -> p g t", p=P, t=PACK))

        zero = keep.tile([P, WIDTH], BF16, name="zero")
        nc.vector.memset(zero[:].bitcast(I32), 0)
        xs_sb = keep.tile([P, N], U8, name="xs_sb", align_bytes=256)
        nc.vector.memset(xs_sb[:].bitcast(I32), 0)
        ws_sb = keep.tile([P, G * H], U8, name="ws_sb", align_bytes=256)
        nc.vector.memset(ws_sb[:].bitcast(I32), 0)
        x_sb = keep.tile([P, 2 * N], U8, name="x_sb", align_bytes=256)
        w_sb = keep.tile([P, G, 2 * H], U8, name="w_sb", align_bytes=256)

        v_rows = v_bytes.rearrange("(g p t) n -> g p t n", p=P, t=PACK)
        u_rows = u.rearrange("(g p t) k -> g p t k", p=P, t=PACK)
        c_rows = c.rearrange("(g p t) k -> g p t k", p=P, t=PACK)
        v_raw, u_raw, c_raw = {}, {}, {}

        def load_v(j, g, tiles=1):
            raw = keep.tile([P, PACK, tiles * WIDTH], U8, name="v_raw_%d_%d" % (j, g), align_bytes=64)
            nc.sync.dma_start(out=raw[:], in_=v_rows[g][:, :, j * WIDTH : (j + tiles) * WIDTH])
            for n in range(tiles):
                v_raw[j + n, g] = raw[:, :, n * WIDTH : (n + 1) * WIDTH]

        def load_u(a):
            u_raw[a] = keep.tile([P, 2, K], BF16, name="u_raw_%d" % a, align_bytes=64)
            nc.sync.dma_start(out=u_raw[a][:], in_=u_rows[a // 2][:, 2 * (a % 2) : 2 * (a % 2) + 2, :])

        def load_c(a):
            c_raw[a] = keep.tile([P, 2, S], BF16, name="c_raw_%d" % a, align_bytes=64)
            nc.sync.dma_start(out=c_raw[a][:], in_=c_rows[a // 2][:, 2 * (a % 2) : 2 * (a % 2) + 2, :])

        def load_x(first, last):
            cols = slice(2 * WIDTH * first, 2 * WIDTH * last)
            nc.sync.dma_start(out=x_sb[:, cols].bitcast(I32), in_=x_words[0][:, cols].bitcast(I32))

        load_v(0, 0)
        load_c(0)
        load_v(0, 1)
        load_u(0)
        load_c(1)
        for q in range(4):
            nc.sync.dma_start(out=xs_sb[32 * q : 32 * q + 4, :].bitcast(I32), in_=x_scales[0][4 * q : 4 * q + 4, :].bitcast(I32))
        load_x(0, 1)
        load_u(1)
        load_c(2)
        load_v(1, 0)
        load_c(3)
        load_u(2)
        load_u(3)
        load_v(1, 1)
        load_v(2, 0, tiles=2)
        load_x(1, TILES)
        load_v(2, 1, tiles=2)
        for q in range(4):
            nc.sync.dma_start(
                out=ws_sb[32 * q : 32 * q + 4, :].bitcast(I32).rearrange("q (g h) -> q g h", g=G),
                in_=w_scales.bitcast(I32).rearrange("g q h -> q g h")[4 * q : 4 * q + 4, :, :],
            )
        nc.sync.dma_start(out=w_sb[:], in_=w_words.rearrange("g p n -> p g n"))

        table = keep.tile([P, 1], F32, name="table")
        nc.gpsimd.memset(table[:], 0.0)
        nc.scalar.activation(out=table[:], in_=table[:], func=ACT.Square)
        warm = out_bank("warm")

        def keep_warm(matmuls):
            for n in range(matmuls):
                nc.tensor.matmul(warm[:], lhsT=zero[:, :P], rhs=zero[:], start=True, stop=True)

        keep_warm(WARM_UPS)
        ident = keep.tile([P, P], F32, name="ident")
        make_identity(nc, ident[:])
        half = keep.tile([P, G, PACK], F32, name="half")
        nc.gpsimd.memset(half[:], 0.5)
        root = keep.tile([P, G, PACK], F32, name="root")
        nc.gpsimd.tensor_tensor(out=root[:], in0=d_sb[:], in1=half[:], op=ALU.pow)

        def quantize(name, grouped, words):
            codes = keep.tile([P, words], U32, name=name, align_bytes=256)
            scales = keep.tile([P, words], U8, name=name + "_scales", align_bytes=256)
            nc.vector.quantize_mx(out=codes[:].bitcast(E4M3X4), scales=scales[:], in_=grouped)
            return codes, scales

        turned, u_grouped, c_grouped, u_mx, c_mx = {}, {}, {}, {}, {}

        def turn(name, a, views):
            turned[name, a] = turn_bank("turned")[:].rearrange("p (b r) -> p b r", b=4)
            for b, view in enumerate(views):
                nc.tensor.transpose(turned[name, a][:, b, :], view, ident[:])

        def turn_u(a, i):
            words = u_raw[a][:, i, :].bitcast(F32)
            turn("u%d" % i, a, [words[:, 256 * g + e : 256 * (g + 1) : 2] for g in range(G) for e in range(2)])

        def turn_c(a):
            turn("c", a, [c_raw[a][:, i, :].bitcast(F32)[:, e:256:2] for i in range(2) for e in range(2)])

        def collect(copy, name, a, dst):
            copy(
                out=dst.bitcast(F32).rearrange("p (b r e) -> p b r e", b=2, e=2),
                in_=turned[name, a].rearrange("p (b e) r -> p b r e", b=2),
            )

        def collect_u(copy, a, i):
            if i == 0:
                u_grouped[a] = work.tile([P, 2 * 2 * P * PACK], BF16, tag="u_grouped", bufs=3, name="u_grouped", align_bytes=64)
            collect(copy, "u%d" % i, a, u_grouped[a][:, 2 * P * PACK * i : 2 * P * PACK * (i + 1)])

        def collect_c(copy, a):
            c_grouped[a] = work.tile([P, 2 * P * PACK], BF16, tag="c_grouped", bufs=3, name="c_grouped", align_bytes=64)
            collect(copy, "c", a, c_grouped[a][:])

        def quantize_u(a):
            u_mx[a] = quantize("u_codes_%d" % a, u_grouped[a][:], 2 * G * P)

        def quantize_c(a):
            c_mx[a] = quantize("c_codes_%d" % a, c_grouped[a][:], 2 * P)

        v_wide, v_grouped, v_mx = {}, {}, {}

        def widen(j, g, planes=range(PACK)):
            way = WIDENERS[j][g]
            if (j, g) not in v_wide:
                v_wide[j, g] = work.tile([P, PACK * WIDTH], BF16, tag="v_wide", bufs=5, name="v_wide", align_bytes=64)
            for s in planes:
                src = v_raw[j, g][:, s, :].bitcast(E4M3)
                scale = vs_sb[:, g, s : s + 1]
                if way == "pairs":
                    dst = v_wide[j, g][:].rearrange("p (r n e) -> p r n e", r=2, e=2)[:, s // 2, :, s % 2]
                else:
                    dst = v_wide[j, g][:].rearrange("p (s n) -> p s n", s=PACK)[:, s, :]
                if way[s] == "S":
                    nc.scalar.activation(out=dst, in_=src, func=ACT.Copy, scale=scale)
                else:
                    nc.vector.tensor_scalar(out=dst, in0=src, scalar1=scale, scalar2=None, op0=ALU.mult)

        def widen_on(engine, j, g):
            way = WIDENERS[j][g]
            widen(j, g, [s for s in range(PACK) if (engine == "V" if way == "pairs" else way[s] == engine)])

        def interleave_v(j, g):
            v_grouped[j, g] = work.tile([P, PACK * WIDTH], BF16, tag="v_grouped", bufs=3, name="v_grouped", align_bytes=64)
            dst, src = v_grouped[j, g][:], v_wide[j, g][:]
            if WIDENERS[j][g] == "pairs":
                nc.vector.tensor_copy(
                    out=dst.bitcast(F32).rearrange("p (n r) -> p n r", r=2),
                    in_=src.bitcast(F32).rearrange("p (r n) -> p n r", r=2),
                )
            else:
                nc.vector.tensor_copy(
                    out=dst.rearrange("p (c i s) -> p c s i", i=4, s=PACK),
                    in_=src.rearrange("p (s c i) -> p c s i", i=4, s=PACK),
                )

        def quantize_v(j, g):
            v_mx[j, g] = quantize("v_codes_%d_%d" % (j, g), v_grouped[j, g][:], WIDTH)

        r_banks = {}

        def residual_cx(j, g, t):
            r_banks[j, g, t] = turn_bank("residual")
            codes, scales = c_mx[2 * g + t // 2]
            rows = slice(P * (t % 2), P * (t % 2 + 1))
            nc.tensor.matmul_mx(
                out=r_banks[j, g, t][:],
                lhsT=codes[:, rows].bitcast(E4M3X4),
                lhsT_scale=scales[:, rows],
                rhs=x_sb[:, 2 * WIDTH * j : 2 * WIDTH * (j + 1)].bitcast(E2M1X4),
                rhs_scale=xs_sb[:, WIDTH * j : WIDTH * (j + 1)],
                start=True,
                stop=False,
            )

        def residual_uv(j, g, t):
            codes, scales = u_mx[2 * g + t // 2]
            for k in range(G):
                rows = slice(P * (G * (t % 2) + k), P * (G * (t % 2) + k + 1))
                v_codes, v_scales = v_mx[j, k]
                nc.tensor.matmul_mx(
                    out=r_banks[j, g, t][:],
                    lhsT=codes[:, rows].bitcast(E4M3X4),
                    lhsT_scale=scales[:, rows],
                    rhs=v_codes[:].bitcast(E4M3X4),
                    rhs_scale=v_scales[:],
                    start=False,
                    stop=(k == G - 1),
                )

        e_wide, e_grouped, e_mx = {}, {}, {}

        def square(j, g, t):
            if (j, g) not in e_wide:
                e_wide[j, g] = work.tile([P, PACK, WIDTH], BF16, tag="e_wide", bufs=4, name="e_wide", align_bytes=64)
            nc.scalar.activation(out=e_wide[j, g][:, t, :], in_=r_banks[j, g, t][:], func=ACT.Square, scale=root[:, g, t : t + 1])

        def halves(j):
            return 2 if j == TILES - 1 else 1

        def interleave_e(j, g, part=0):
            cols = WIDTH // halves(j)
            e_grouped[j, g, part] = work.tile([P, cols * PACK], BF16, tag="e_grouped", bufs=3, name="e_grouped", align_bytes=64)
            nc.vector.tensor_copy(
                out=e_grouped[j, g, part][:].rearrange("p (c i t) -> p c t i", i=4, t=PACK),
                in_=e_wide[j, g][:, :, part * cols : (part + 1) * cols].rearrange("p t (c i) -> p c t i", i=4),
            )

        def quantize_e(j, g, part=0):
            e_mx[j, g, part] = quantize("e_codes_%d_%d_%d" % (j, g, part), e_grouped[j, g, part][:], WIDTH // halves(j))

        o_banks = {}

        def contrast(j, q):
            o_banks[j, q] = out_bank("contrasts")
            part, n = divmod(q, WIDTH // halves(j) // P)
            for g in range(G):
                codes, scales = e_mx[j, g, part]
                nc.tensor.matmul_mx(
                    out=o_banks[j, q][:],
                    lhsT=codes[:, P * n : P * (n + 1)].bitcast(E4M3X4),
                    lhsT_scale=scales[:, P * n : P * (n + 1)],
                    rhs=w_sb[:, g, :].bitcast(E2M1X4),
                    rhs_scale=ws_sb[:, H * g : H * (g + 1)],
                    start=(g == 0),
                    stop=(g == G - 1),
                )

        def store(j, q, copy):
            o_sb = work.tile([P, H], F32, tag="o_sb", bufs=6, name="o_sb", align_bytes=64)
            copy(out=o_sb[:], in_=o_banks[j, q][:])
            row = WIDTH * j + P * q
            nc.sync.dma_start(out=out[row : row + P, :], in_=o_sb[:])

        by_scalar, by_vector = nc.scalar.copy, nc.vector.tensor_copy

        widen(0, 1)
        widen(0, 0, range(0, 3))
        turn_c(0)
        collect_c(by_vector, 0)
        widen(0, 0, range(3, 4))
        keep_warm(2)
        turn_u(0, 0)
        turn_u(0, 1)
        collect_u(by_scalar, 0, 0)
        collect_u(by_scalar, 0, 1)
        quantize_c(0)
        interleave_v(0, 0)
        interleave_v(0, 1)
        turn_c(1)
        collect_c(by_scalar, 1)
        residual_cx(0, 0, 0)
        residual_cx(0, 0, 1)
        turn_u(1, 0)
        collect_u(by_scalar, 1, 0)
        turn_c(2)
        collect_c(by_scalar, 2)
        turn_u(1, 1)
        collect_u(by_scalar, 1, 1)
        quantize_u(0)
        quantize_v(0, 0)
        quantize_v(0, 1)
        widen(1, 0)
        for t in range(2):
            residual_uv(0, 0, t)
            square(0, 0, t)
        quantize_u(1)
        quantize_c(1)
        turn_c(3)
        collect_c(by_vector, 3)
        for a in (2, 3):
            for i in range(2):
                turn_u(a, i)
                collect_u(by_scalar, a, i)
        widen(1, 1)
        quantize_c(2)
        quantize_u(2)
        quantize_c(3)
        interleave_v(1, 0)
        quantize_u(3)
        interleave_v(1, 1)
        for g, t in ((0, 2), (0, 3), (1, 0), (1, 1), (1, 2), (1, 3)):
            residual_cx(0, g, t)
            residual_uv(0, g, t)
            square(0, g, t)
        for g in range(G):
            quantize_v(1, g)

        for g in range(G):
            widen(2, g)
        for j in range(1, TILES):
            if j == 1:
                for g in range(G):
                    widen_on("S", 3, g)
            for g in range(G):
                for t in range(PACK):
                    if g == 1 and j >= 2:
                        contrast(j - 2, t)
                        store(j - 2, t, by_scalar)
                    residual_cx(j, g, t)
                    residual_uv(j, g, t)
                    square(j, g, t)
            if j + 1 < TILES:
                interleave_v(j + 1, 0)
                interleave_v(j + 1, 1)
            interleave_e(j - 1, 0)
            if j + 1 < TILES:
                quantize_v(j + 1, 0)
                quantize_v(j + 1, 1)
            quantize_e(j - 1, 0)
            interleave_e(j - 1, 1)
            if j == 1:
                for g in range(G):
                    widen_on("V", 3, g)
            quantize_e(j - 1, 1)

        last = TILES - 1
        for q in range(WIDTH // P):
            contrast(last - 1, q)
            store(last - 1, q, by_scalar)
        for g in range(G):
            for part in range(2):
                interleave_e(last, g, part)
                quantize_e(last, g, part)
        for q in range(WIDTH // P):
            contrast(last, q)
            store(last, q, [by_scalar, by_vector][q % 2])
